import numpy as np
import ml_dtypes


def mxq(x, axis, fmt="e4m3"):
    dtype, down = {"e4m3": (ml_dtypes.float8_e4m3fn, 7), "e5m2": (ml_dtypes.float8_e5m2, 14)}[fmt]
    v = np.moveaxis(np.asarray(x, np.float32).astype(ml_dtypes.bfloat16).astype(np.float64), axis, -1)
    blocks = v.reshape(v.shape[:-1] + (-1, 32))
    amax = np.abs(blocks).max(-1, keepdims=True)
    byte = np.maximum(np.where(amax > 0, np.frexp(amax)[1] - 1 + 127, 0) - down, 1)
    scale = np.exp2(byte - 127.0)
    codes = (blocks / scale).astype(np.float32).astype(dtype).astype(np.float64)
    return np.moveaxis((codes * scale).reshape(v.shape), -1, axis)


WIDE = False


def mx_kscale(k):
    if not WIDE:
        return np.ones(k)
    levels = np.array([10, -10, 5, -5, 0])
    if k % 512:
        return np.exp2(np.random.permutation(np.resize(levels, k // 32))).repeat(32)
    a = np.empty((k // 512, 16))
    for p in range(k // 512):
        a[p, :8] = np.random.permutation(np.resize(levels, 8))
        for g in range(8):
            far = levels[np.abs(levels - a[p, g]) >= 10]
            a[p, g + 8] = far[np.random.randint(len(far))]
    return np.exp2(a.ravel()).repeat(32)


def f64(x):
    return np.asarray(x).astype(np.float64)


def striped(idx):
    return np.tile(idx.reshape(-1, 16).T, (8, 1)).astype(np.uint16)


def unstriped(offs):
    return offs[:16].T.reshape(-1).astype(np.int64)


def pack_weight(w):
    k, n = w.shape
    w = f64(np.asarray(w, np.float32).astype(ml_dtypes.bfloat16)).reshape(k // 32, 32, n)
    amax = np.abs(w).max(1)
    byte = np.clip(np.where(amax > 0, np.frexp(amax)[1] - 1 + 127 - 7, 1), 1, 254)
    scaled = (w * np.exp2(127.0 - byte)[:, None, :]).reshape(k, n).astype(np.float32)
    words = np.ascontiguousarray(scaled.reshape(k // 512, 128, 4, n).transpose(0, 1, 3, 2)).astype(ml_dtypes.float8_e4m3fn).view(np.uint8)
    return words, np.ascontiguousarray(byte.astype(np.uint8).reshape(k // 512, 16, n))


def unpack_weight(words, scales):
    g, p, n, _ = words.shape
    vals = np.ascontiguousarray(words).view(ml_dtypes.float8_e4m3fn).astype(np.float64) * np.repeat(np.exp2(scales.astype(np.float64) - 127.0), 8, axis=1)[..., None]
    return vals.transpose(0, 1, 3, 2).reshape(g * 512, n)


E2M1 = np.array([0.0, 0.5, 1.0, 1.5, 2.0, 3.0, 4.0, 6.0, -0.0, -0.5, -1.0, -1.5, -2.0, -3.0, -4.0, -6.0])


def pack_fp4(w):
    k, n = w.shape
    w = f64(np.asarray(w, np.float32).astype(ml_dtypes.bfloat16)).reshape(k // 32, 32, n)
    amax = np.abs(w).max(1)
    mant, ex = np.frexp(amax / 6.0)
    byte = np.clip(np.where(amax > 0, np.where(mant > 0.5, ex, ex - 1) + 127, 1), 1, 254)
    scaled = (w * np.exp2(127.0 - byte)[:, None, :]).reshape(k, n).astype(np.float32)
    c = np.ascontiguousarray(scaled.reshape(k // 512, 128, 4, n).transpose(0, 1, 3, 2)).astype(ml_dtypes.float4_e2m1fn).view(np.uint8) & 0xF
    words = (c[..., 0::2] | (c[..., 1::2] << 4)).reshape(k // 512, 128, 2 * n)
    return np.ascontiguousarray(words), np.ascontiguousarray(byte.astype(np.uint8).reshape(k // 512, 16, n))


def unpack_fp4(words, scales):
    g, _, n = scales.shape
    words = np.ascontiguousarray(words).reshape(g, 128, n, 2)
    nib = np.empty((g, 128, n, 4), np.uint8)
    nib[..., 0::2] = words & 0xF
    nib[..., 1::2] = words >> 4
    vals = E2M1[nib] * np.repeat(np.exp2(scales.astype(np.float64) - 127.0), 8, axis=1)[..., None]
    return vals.transpose(0, 1, 3, 2).reshape(g * 512, n)


def planes(y):
    n, m = y.shape
    v = y.astype(np.float32).astype(ml_dtypes.bfloat16).astype(np.float64).reshape(n // 32, 32, m)
    top = np.abs(v).max(1)
    byte = np.clip(np.where(top > 0, np.frexp(top)[1] - 1 + 127 - 7, 1), 1, 254)
    codes = (v * np.exp2(127.0 - byte)[:, None, :]).reshape(n, m).astype(np.float32).astype(ml_dtypes.float8_e4m3fn).view(np.uint8)
    words = codes.reshape(n // 512, 128, 4, m).transpose(0, 1, 3, 2)
    return np.ascontiguousarray(words), np.ascontiguousarray(byte.astype(np.uint8).reshape(n // 512, 16, m))


def sigmoid(v):
    return 1.0 / (1.0 + np.exp(-np.maximum(v, -700.0)))


K, T, S, N, H = 1024, 1024, 512, 512, 512


def setup_inputs():
    n = np.random.standard_normal
    s = mx_kscale(K)[:, None]
    u = mx_kscale(H)
    packed_xT = pack_weight(n((K, T)) * s)
    packed_w1 = pack_fp4(n((K, N)) / np.sqrt(K) / s)
    packed_w2 = pack_fp4(n((K, N)) / np.sqrt(K) / s)
    packed_w3 = pack_fp4(n((H, N)) / np.sqrt(H) / u[:, None])
    return {
        "x_words": packed_xT[0],
        "x_scales": packed_xT[1],
        "w1_words": packed_w1[0],
        "w1_scales": packed_w1[1],
        "w2_words": packed_w2[0],
        "w2_scales": packed_w2[1],
        "unit": (np.random.uniform(0.6, 1.4, (H, 1)) * u[:, None]).astype(np.float32),
        "w3_words": packed_w3[0],
        "w3_scales": packed_w3[1],
        "offs": striped(np.random.permutation(T)[:S]),
        "p1": striped(np.random.permutation(S)),
        "p2": striped(np.random.permutation(S)),
        "p3": striped(np.random.permutation(S)),
    }


def reference(x_words, x_scales, w1_words, w1_scales, w2_words, w2_scales, unit, w3_words, w3_scales, offs, p1, p2, p3):
    xq = unpack_weight(x_words, x_scales)[:, unstriped(offs)]
    y = unpack_fp4(w1_words, w1_scales).T @ xq
    yw = unpack_fp4(w2_words, w2_scales).T @ xq
    dec = sigmoid(yw)
    y1 = y[:, unstriped(p1)]
    up1 = y + dec * y1
    ap = dec[:, unstriped(p1)]
    dec2 = dec * ap
    x12 = up1[:, unstriped(p2)]
    up2_ = up1 + dec2 * x12
    x13 = up1[:, unstriped(p3)]
    hid = f64(unit) * np.maximum(up2_, x13)
    out_0 = unpack_fp4(w3_words, w3_scales).T @ mxq(hid, 0, "e4m3")
    return (out_0,) + planes(out_0)

@@ -1,0 +1,215 @@
+from contextlib import ExitStack
+
+import concourse.mybir as mybir
+
+K, T, S, N, H = 1024, 1024, 512, 512, 512
+FLOPS = 2 * (2 * K * N * S) + 2 * H * N * S
+
+F32 = mybir.dt.float32
+BF16 = mybir.dt.bfloat16
+I32 = mybir.dt.int32
+U32 = mybir.dt.uint32
+U16 = mybir.dt.uint16
+U8 = mybir.dt.uint8
+FP8X4 = mybir.dt.float8_e4m3fn_x4
+FP4X4 = mybir.dt.float4_e2m1fn_x4
+ALU = mybir.AluOpType
+ACT = mybir.ActivationFunctionType
+
+P = 128
+PACK = 4
+PASSES = K // (P * PACK)
+HALF = S // 2
+CHUNK = 128
+CHUNKS = S // CHUNK
+RUN = 4
+
+
+def entries(lst, start, count):
+    return lst[:, start // 16 : (start + count) // 16]
+
+
+def load_scales(nc, tile, scales):
+    for q in range(4):
+        nc.sync.dma_start(
+            out=tile[32 * q : 32 * q + 4, :, :].bitcast(I32),
+            in_=scales[:, 4 * q : 4 * q + 4, :].rearrange("o r n -> r o n").bitcast(I32),
+        )
+
+
+def woven(tile):
+    return tile.rearrange("p (c i t) -> p c t i", i=RUN, t=PACK)
+
+
+def planes(ap):
+    return ap.rearrange("p t (c i) -> p c t i", i=RUN)
+
+
+def tile_picked_yptrjmp_max_po_kernel(
+    tc, x_words, x_scales, w1_words, w1_scales, w2_words, w2_scales, unit, w3_words, w3_scales,
+    offs, p1, p2, p3, out_0, out_1, out_2,
+):
+    nc = tc.nc
+    with ExitStack() as ctx:
+        keep = ctx.enter_context(tc.tile_pool(name="keep", bufs=1))
+        ring = ctx.enter_context(tc.tile_pool(name="ring", bufs=2))
+        psum = ctx.enter_context(tc.psum_pool(name="psum", bufs=8))
+
+        lists = {}
+        for name in ("offs", "p1", "p2", "p3"):
+            lists[name] = keep.tile([P, S // 16], U16, name="list_" + name)
+
+        def weight_tiles(name, passes):
+            raw_words = keep.tile([P, passes, 2 * N], U8, name=name + "_raw_words")
+            raw_scales = keep.tile([P, passes, N], U8, name=name + "_raw_scales")
+            words = keep.tile([P, passes, PACK, 2 * P], U8, name=name + "_words", align_bytes=64)
+            scales = keep.tile([P, passes, PACK, P], U8, name=name + "_scales", align_bytes=64)
+            return raw_words, raw_scales, words, scales
+
+        w1 = weight_tiles("w1", PASSES)
+        w2 = weight_tiles("w2", PASSES)
+        w3 = weight_tiles("w3", 1)
+        table_words = [keep.tile([P, T], I32, name="table_words%d" % o) for o in range(PASSES)]
+        table_scales = keep.tile([P, PASSES, T], U8, name="table_scales")
+
+        def load_weight(w, words, scales):
+            nc.vector.memset(w[1][:].bitcast(I32), 0)
+            nc.sync.dma_start(out=w[0][:].bitcast(I32), in_=words.rearrange("o p b -> p o b").bitcast(I32))
+            load_scales(nc, w[1], scales)
+
+        def deal_weight(w):
+            nc.vector.tensor_copy(
+                out=w[2][:].rearrange("p o t (m b) -> p o t m b", b=2),
+                in_=w[0][:].rearrange("p o (m t b) -> p o t m b", t=PACK, b=2),
+            )
+            nc.vector.tensor_copy(out=w[3][:], in_=w[1][:].rearrange("p o (m t) -> p o t m", t=PACK))
+
+        def load_table_words(o):
+            nc.sync.dma_start(out=table_words[o][:], in_=x_words[o].rearrange("p c r -> p (c r)").bitcast(I32))
+
+        load_weight(w1, w1_words, w1_scales)
+        load_weight(w2, w2_words, w2_scales)
+        nc.sync.dma_start(lists["offs"][:], offs)
+        load_table_words(0)
+        nc.vector.memset(table_scales[:].bitcast(I32), 0)
+        load_scales(nc, table_scales, x_scales)
+        load_table_words(1)
+        unit_sb = keep.tile([P, PACK], F32, name="unit_sb")
+        nc.sync.dma_start(out=unit_sb[:], in_=unit.rearrange("(p t) o -> p (t o)", t=PACK))
+        nc.sync.dma_start(lists["p1"][:], p1)
+        load_weight(w3, w3_words, w3_scales)
+        nc.sync.dma_start(lists["p2"][:], p2)
+        nc.sync.dma_start(lists["p3"][:], p3)
+
+        deal_weight(w1)
+        deal_weight(w2)
+
+        unit_abs = keep.tile([P, PACK], F32, name="unit_abs")
+        unit_sign = keep.tile([P, CHUNK, PACK], BF16, name="unit_sign")
+        nc.scalar.activation(unit_abs[:], unit_sb[:], ACT.Abs)
+        nc.scalar.activation(unit_sign[:], unit_sb[:].unsqueeze(1).to_broadcast([P, CHUNK, PACK]), ACT.Sign)
+
+        picked_words = keep.tile([P, PASSES, S], U32, name="picked_words", align_bytes=64)
+        picked_scales = keep.tile([P, PASSES, S], U8, name="picked_scales", align_bytes=64)
+        y = [keep.tile([P, S], F32, name="y%d" % t) for t in range(PACK)]
+        dec = keep.tile([P, PACK, S], F32, name="dec")
+        ap = keep.tile([P, PACK, S], F32, name="ap")
+        up1 = keep.tile([P, PACK, S], F32, name="up1")
+
+        for h in range(2):
+            cols = slice(h * HALF, (h + 1) * HALF)
+            picks = entries(lists["offs"], h * HALF, HALF)
+            nc.vector.tensor_copy(picked_words[:, 0, cols], table_words[0][:].bitcast(U32).indirect(picks))
+            for o in range(PASSES):
+                nc.vector.tensor_copy(picked_scales[:, o, cols], table_scales[:, o, :].indirect(picks))
+            nc.vector.tensor_copy(picked_words[:, 1, cols], table_words[1][:].bitcast(U32).indirect(picks))
+            for t in range(PACK):
+                bank = psum.tile([P, 2, HALF], F32, name="bank")
+                for slot, w in enumerate((w2, w1)):
+                    for o in range(PASSES):
+                        nc.tensor.matmul_mx(
+                            out=bank[:, slot, :],
+                            lhsT=w[2][:, o, t, :].bitcast(FP4X4),
+                            lhsT_scale=w[3][:, o, t, :],
+                            rhs=picked_words[:, o, cols].bitcast(FP8X4),
+                            rhs_scale=picked_scales[:, o, cols],
+                            start=(o == 0),
+                            stop=(o == PASSES - 1),
+                        )
+                nc.scalar.activation(dec[:, t, cols], bank[:, 0, :], ACT.Sigmoid)
+                nc.scalar.activation(y[t][:, cols], bank[:, 1, :], ACT.Copy, scale=unit_abs[:, t : t + 1])
+
+        deal_weight(w3)
+
+        for t in range(PACK):
+            m1 = ring.tile([P, S], F32, name="m1")
+            for h in range(2):
+                cols = slice(h * HALF, (h + 1) * HALF)
+                picks = entries(lists["p1"], h * HALF, HALF)
+                nc.vector.tensor_tensor(m1[:, cols], y[t][:].indirect(picks), dec[:, t, cols], ALU.mult)
+                nc.scalar.activation(ap[:, t, cols], dec[:, t, :].indirect(picks), ACT.Copy)
+            nc.vector.tensor_tensor(up1[:, t, :], m1[:], y[t][:], ALU.add)
+
+        out_words = keep.tile([P, S], I32, name="out_words", align_bytes=64)
+        out_scales = keep.tile([P, S], U8, name="out_scales", align_bytes=64)
+        out_rows = out_0.rearrange("(p t) j -> p t j", t=PACK)
+        results = {}
+
+        def hidden(c):
+            cols = slice(c * CHUNK, (c + 1) * CHUNK)
+            x12 = ring.tile([P, PACK, CHUNK], F32, name="x12")
+            x13 = ring.tile([P, PACK, CHUNK], F32, name="x13")
+            for fetched, name in ((x12, "p2"), (x13, "p3")):
+                picks = entries(lists[name], c * CHUNK, CHUNK)
+                for t in range(PACK):
+                    nc.scalar.activation(fetched[:, t, :], up1[:, t, :].indirect(picks), ACT.Copy)
+            dec2 = ring.tile([P, PACK, CHUNK], F32, name="dec2")
+            m2 = ring.tile([P, PACK, CHUNK], F32, name="m2")
+            up2 = ring.tile([P, PACK, CHUNK], F32, name="up2")
+            top = ring.tile([P, CHUNK * PACK], BF16, name="top")
+            hid = ring.tile([P, CHUNK * PACK], BF16, name="hid", align_bytes=64)
+            hid_words = ring.tile([P, CHUNK], U32, name="hid_words", align_bytes=64)
+            hid_scales = ring.tile([P, CHUNK], U8, name="hid_scales", align_bytes=64)
+            nc.vector.tensor_tensor(dec2[:], dec[:, :, cols], ap[:, :, cols], ALU.mult)
+            nc.vector.tensor_tensor(m2[:], dec2[:], x12[:], ALU.mult)
+            nc.vector.tensor_tensor(up2[:], m2[:], up1[:, :, cols], ALU.add)
+            nc.vector.tensor_tensor(woven(top[:]), planes(up2[:]), planes(x13[:]), ALU.max)
+            nc.vector.tensor_tensor(hid[:], top[:], unit_sign[:].rearrange("p c t -> p (c t)"), ALU.mult)
+            nc.vector.quantize_mx(out=hid_words[:].bitcast(FP8X4), scales=hid_scales[:], in_=hid[:])
+            bank = psum.tile([P, PACK, CHUNK], F32, name="bank")
+            for t in range(PACK):
+                nc.tensor.matmul_mx(
+                    out=bank[:, t, :],
+                    lhsT=w3[2][:, 0, t, :].bitcast(FP4X4),
+                    lhsT_scale=w3[3][:, 0, t, :],
+                    rhs=hid_words[:].bitcast(FP8X4),
+                    rhs_scale=hid_scales[:],
+                    start=True,
+                    stop=True,
+                )
+            result = keep.tile([P, PACK, CHUNK], F32, name="result%d" % c)
+            nc.scalar.activation(result[:], bank[:], ACT.Copy)
+            nc.sync.dma_start(out=out_rows[:, :, cols], in_=result[:])
+            results[c] = result
+
+        def hand_on(c):
+            cols = slice(c * CHUNK, (c + 1) * CHUNK)
+            rounded = ring.tile([P, CHUNK * PACK], BF16, name="rounded", align_bytes=64)
+            nc.vector.tensor_copy(out=woven(rounded[:]), in_=planes(results[c][:]))
+            nc.vector.quantize_mx(out=out_words[:, cols].bitcast(FP8X4), scales=out_scales[:, cols], in_=rounded[:])
+            nc.sync.dma_start(
+                out=out_1[0].rearrange("p c r -> p (c r)").bitcast(I32)[:, cols], in_=out_words[:, cols]
+            )
+
+        lag = 2
+        for c in range(CHUNKS + lag):
+            if c < CHUNKS:
+                hidden(c)
+            if c >= lag:
+                hand_on(c - lag)
+        for q in range(4):
+            queue = nc.sync if q % 2 == 0 else nc.scalar
+            queue.dma_start(
+                out=out_2[0, 4 * q : 4 * q + 4, :].bitcast(I32),
+                in_=out_scales[32 * q : 32 * q + 4, :].bitcast(I32),
+            )

@@ -23,6 +23,7 @@ HALF = S // 2
 CHUNK = 128
 CHUNKS = S // CHUNK
 RUN = 4
+ORDER = (1, 2, 3, 0)
 
 
 def entries(lst, start, count):
@@ -32,7 +33,7 @@ def entries(lst, start, count):
 def load_scales(nc, tile, scales):
     for q in range(4):
         nc.sync.dma_start(
-            out=tile[32 * q : 32 * q + 4, :, :].bitcast(I32),
+            out=tile[32 * q : 32 * q + 4].bitcast(I32),
             in_=scales[:, 4 * q : 4 * q + 4, :].rearrange("o r n -> r o n").bitcast(I32),
         )
 
@@ -59,154 +60,256 @@ def tile_picked_yptrjmp_max_po_kernel(
         for name in ("offs", "p1", "p2", "p3"):
             lists[name] = keep.tile([P, S // 16], U16, name="list_" + name)
 
-        def weight_tiles(name, passes):
-            raw_words = keep.tile([P, passes, 2 * N], U8, name=name + "_raw_words")
-            raw_scales = keep.tile([P, passes, N], U8, name=name + "_raw_scales")
-            words = keep.tile([P, passes, PACK, 2 * P], U8, name=name + "_words", align_bytes=64)
-            scales = keep.tile([P, passes, PACK, P], U8, name=name + "_scales", align_bytes=64)
-            return raw_words, raw_scales, words, scales
-
-        w1 = weight_tiles("w1", PASSES)
-        w2 = weight_tiles("w2", PASSES)
-        w3 = weight_tiles("w3", 1)
+        raw_words = [keep.tile([P, PASSES, 2 * N], U8, name="raw_words%d" % w) for w in range(2)]
+        raw_scales = [keep.tile([P, PASSES, N], U8, name="raw_scales%d" % w) for w in range(2)]
+        raw3_words = keep.tile([P, 1, 2 * N], U8, name="raw3_words")
+        raw3_scales = keep.tile([P, 1, N], U8, name="raw3_scales")
         table_words = [keep.tile([P, T], I32, name="table_words%d" % o) for o in range(PASSES)]
         table_scales = keep.tile([P, PASSES, T], U8, name="table_scales")
 
-        def load_weight(w, words, scales):
-            nc.vector.memset(w[1][:].bitcast(I32), 0)
-            nc.sync.dma_start(out=w[0][:].bitcast(I32), in_=words.rearrange("o p b -> p o b").bitcast(I32))
-            load_scales(nc, w[1], scales)
-
-        def deal_weight(w):
-            nc.vector.tensor_copy(
-                out=w[2][:].rearrange("p o t (m b) -> p o t m b", b=2),
-                in_=w[0][:].rearrange("p o (m t b) -> p o t m b", t=PACK, b=2),
-            )
-            nc.vector.tensor_copy(out=w[3][:], in_=w[1][:].rearrange("p o (m t) -> p o t m", t=PACK))
+        def load_words(tile, words):
+            nc.sync.dma_start(out=tile.bitcast(I32), in_=words.rearrange("o p b -> p o b").bitcast(I32))
 
         def load_table_words(o):
             nc.sync.dma_start(out=table_words[o][:], in_=x_words[o].rearrange("p c r -> p (c r)").bitcast(I32))
 
-        load_weight(w1, w1_words, w1_scales)
-        load_weight(w2, w2_words, w2_scales)
-        nc.sync.dma_start(lists["offs"][:], offs)
-        load_table_words(0)
         nc.vector.memset(table_scales[:].bitcast(I32), 0)
-        load_scales(nc, table_scales, x_scales)
+        for w in range(2):
+            nc.vector.memset(raw_scales[w][:].bitcast(I32), 0)
+        nc.vector.memset(raw3_scales[:].bitcast(I32), 0)
+        nc.sync.dma_start(lists["offs"][:], offs)
+        load_scales(nc, table_scales[:], x_scales)
+        load_table_words(0)
+        load_words(raw_words[0][:], w2_words)
         load_table_words(1)
+        load_scales(nc, raw_scales[0][:], w2_scales)
+        load_words(raw_words[1][:], w1_words)
+        load_scales(nc, raw_scales[1][:], w1_scales)
         unit_sb = keep.tile([P, PACK], F32, name="unit_sb")
         nc.sync.dma_start(out=unit_sb[:], in_=unit.rearrange("(p t) o -> p (t o)", t=PACK))
         nc.sync.dma_start(lists["p1"][:], p1)
-        load_weight(w3, w3_words, w3_scales)
+        load_words(raw3_words[:], w3_words)
+        load_scales(nc, raw3_scales[:], w3_scales)
         nc.sync.dma_start(lists["p2"][:], p2)
         nc.sync.dma_start(lists["p3"][:], p3)
 
-        deal_weight(w1)
-        deal_weight(w2)
-
         unit_abs = keep.tile([P, PACK], F32, name="unit_abs")
         unit_sign = keep.tile([P, CHUNK, PACK], BF16, name="unit_sign")
-        nc.scalar.activation(unit_abs[:], unit_sb[:], ACT.Abs)
-        nc.scalar.activation(unit_sign[:], unit_sb[:].unsqueeze(1).to_broadcast([P, CHUNK, PACK]), ACT.Sign)
+        twice_positive = keep.tile([P, PACK], F32, name="twice_positive")
+        nc.gpsimd.tensor_scalar(twice_positive[:], unit_sb[:], 0.0, 2.0, ALU.is_ge, ALU.mult)
+        nc.gpsimd.tensor_scalar(
+            unit_sign[:], twice_positive[:].unsqueeze(1).to_broadcast([P, CHUNK, PACK]), 1.0, -1.0, ALU.mult, ALU.add
+        )
+        nc.gpsimd.tensor_tensor(unit_abs[:], unit_sb[:], unit_sign[:, 0, :], ALU.mult)
 
-        picked_words = keep.tile([P, PASSES, S], U32, name="picked_words", align_bytes=64)
-        picked_scales = keep.tile([P, PASSES, S], U8, name="picked_scales", align_bytes=64)
-        y = [keep.tile([P, S], F32, name="y%d" % t) for t in range(PACK)]
+        picked_words = [keep.tile([P, S], U32, name="picked_words%d" % o, tag="after_products%d" % o, align_bytes=64) for o in range(PASSES)]
+        picked_scales = [keep.tile([P, S], U8, name="picked_scales%d" % o, align_bytes=64) for o in range(PASSES)]
+        y = [keep.tile([P, S], F32, name="y%d" % t, tag="y%d" % t) for t in range(PACK)]
+        m1 = [keep.tile([P, S], F32, name="m1_%d" % t, tag="m1_%d" % t) for t in range(PACK)]
         dec = keep.tile([P, PACK, S], F32, name="dec")
-        ap = keep.tile([P, PACK, S], F32, name="ap")
-        up1 = keep.tile([P, PACK, S], F32, name="up1")
+        ap = {0: keep.tile([P, PACK, HALF], F32, name="ap0")}
+        up1_flat = keep.tile([P, PACK * S], F32, name="up1")
+        up1 = up1_flat[:].rearrange("p (t j) -> p t j", t=PACK)
+        dealt = {}
 
-        for h in range(2):
+        def deal(w, ts):
+            name = "%d_%d" % (w, ts.start)
+            count = ts.stop - ts.start
+            words = keep.tile([P, count, PASSES, 2 * P], U8, name="dealt_words" + name, align_bytes=64)
+            scales = keep.tile([P, count, PASSES, P], U8, name="dealt_scales" + name, align_bytes=64)
+            nc.vector.tensor_copy(
+                out=words[:].bitcast(U16).rearrange("p t o m -> p o t m"),
+                in_=raw_words[w][:].bitcast(U16).rearrange("p o (m t) -> p o t m", t=PACK)[:, :, ts, :],
+            )
+            nc.vector.tensor_copy(
+                out=scales[:].rearrange("p t o m -> p o t m"),
+                in_=raw_scales[w][:].rearrange("p o (m t) -> p o t m", t=PACK)[:, :, ts, :],
+            )
+            for t in range(ts.start, ts.stop):
+                dealt[t, w] = (words[:, t - ts.start], scales[:, t - ts.start])
+
+        w3_dealt_words = keep.tile([P, PACK, 2 * P], U8, name="w3_dealt_words", align_bytes=64)
+        w3_dealt_scales = keep.tile([P, PACK, P], U8, name="w3_dealt_scales", align_bytes=64)
+
+        def deal_w3():
+            nc.vector.tensor_copy(
+                out=w3_dealt_words[:].bitcast(U16),
+                in_=raw3_words[:, 0, :].bitcast(U16).rearrange("p (m t) -> p t m", t=PACK),
+            )
+            nc.vector.tensor_copy(
+                out=w3_dealt_scales[:], in_=raw3_scales[:, 0, :].rearrange("p (m t) -> p t m", t=PACK)
+            )
+
+        def pick_words(o):
+            nc.vector.tensor_copy(picked_words[o][:], table_words[o][:].bitcast(U32).indirect(lists["offs"][:]))
+
+        def pick_scales(o):
+            nc.vector.tensor_copy(picked_scales[o][:], table_scales[:, o, :].indirect(lists["offs"][:]))
+
+        banks = {}
+
+        def product_pass(t, w, o):
+            words, scales = dealt[t, w]
+            if o == 0:
+                banks[t, w] = psum.tile([P, S], F32, name="bank")
+            nc.tensor.matmul_mx(
+                out=banks[t, w][:],
+                lhsT=words[:, o, :].bitcast(FP4X4),
+                lhsT_scale=scales[:, o, :],
+                rhs=picked_words[o][:].bitcast(FP8X4),
+                rhs_scale=picked_scales[o][:],
+                start=(o == 0),
+                stop=(o == PASSES - 1),
+            )
+
+        def leave_psum(t):
+            nc.scalar.activation(dec[:, t, :], banks[t, 0][:], ACT.Sigmoid)
+            nc.scalar.activation(y[t][:], banks[t, 1][:], ACT.Copy, scale=unit_abs[:, t : t + 1])
+
+        def parent_product(t, h):
             cols = slice(h * HALF, (h + 1) * HALF)
-            picks = entries(lists["offs"], h * HALF, HALF)
-            nc.vector.tensor_copy(picked_words[:, 0, cols], table_words[0][:].bitcast(U32).indirect(picks))
-            for o in range(PASSES):
-                nc.vector.tensor_copy(picked_scales[:, o, cols], table_scales[:, o, :].indirect(picks))
-            nc.vector.tensor_copy(picked_words[:, 1, cols], table_words[1][:].bitcast(U32).indirect(picks))
-            for t in range(PACK):
-                bank = psum.tile([P, 2, HALF], F32, name="bank")
-                for slot, w in enumerate((w2, w1)):
-                    for o in range(PASSES):
-                        nc.tensor.matmul_mx(
-                            out=bank[:, slot, :],
-                            lhsT=w[2][:, o, t, :].bitcast(FP4X4),
-                            lhsT_scale=w[3][:, o, t, :],
-                            rhs=picked_words[:, o, cols].bitcast(FP8X4),
-                            rhs_scale=picked_scales[:, o, cols],
-                            start=(o == 0),
-                            stop=(o == PASSES - 1),
-                        )
-                nc.scalar.activation(dec[:, t, cols], bank[:, 0, :], ACT.Sigmoid)
-                nc.scalar.activation(y[t][:, cols], bank[:, 1, :], ACT.Copy, scale=unit_abs[:, t : t + 1])
+            picks = entries(lists["p1"], h * HALF, HALF)
+            nc.vector.tensor_tensor(m1[t][:, cols], y[t][:].indirect(picks), dec[:, t, cols], ALU.mult)
 
-        deal_weight(w3)
+        def parent_decay(t, h):
+            picks = entries(lists["p1"], h * HALF, HALF)
+            nc.scalar.activation(ap[h][:, t, :], dec[:, t, :].indirect(picks), ACT.Copy)
 
-        for t in range(PACK):
-            m1 = ring.tile([P, S], F32, name="m1")
-            for h in range(2):
-                cols = slice(h * HALF, (h + 1) * HALF)
-                picks = entries(lists["p1"], h * HALF, HALF)
-                nc.vector.tensor_tensor(m1[:, cols], y[t][:].indirect(picks), dec[:, t, cols], ALU.mult)
-                nc.scalar.activation(ap[:, t, cols], dec[:, t, :].indirect(picks), ACT.Copy)
-            nc.vector.tensor_tensor(up1[:, t, :], m1[:], y[t][:], ALU.add)
+        def first_sum(t):
+            nc.vector.tensor_tensor(up1[:, t, :], m1[t][:], y[t][:], ALU.add)
 
         out_words = keep.tile([P, S], I32, name="out_words", align_bytes=64)
         out_scales = keep.tile([P, S], U8, name="out_scales", align_bytes=64)
         out_rows = out_0.rearrange("(p t) j -> p t j", t=PACK)
-        results = {}
+        first, last = ORDER[0], ORDER[-1]
+        x12, x13, dec2, m2, up2, top, hid, results, rounded = {}, {}, {}, {}, {}, {}, {}, {}, {}
 
-        def hidden(c):
-            cols = slice(c * CHUNK, (c + 1) * CHUNK)
-            x12 = ring.tile([P, PACK, CHUNK], F32, name="x12")
-            x13 = ring.tile([P, PACK, CHUNK], F32, name="x13")
-            for fetched, name in ((x12, "p2"), (x13, "p3")):
-                picks = entries(lists[name], c * CHUNK, CHUNK)
-                for t in range(PACK):
-                    nc.scalar.activation(fetched[:, t, :], up1[:, t, :].indirect(picks), ACT.Copy)
-            dec2 = ring.tile([P, PACK, CHUNK], F32, name="dec2")
-            m2 = ring.tile([P, PACK, CHUNK], F32, name="m2")
-            up2 = ring.tile([P, PACK, CHUNK], F32, name="up2")
-            top = ring.tile([P, CHUNK * PACK], BF16, name="top")
-            hid = ring.tile([P, CHUNK * PACK], BF16, name="hid", align_bytes=64)
+        def chunk(c):
+            return slice(c * CHUNK, (c + 1) * CHUNK)
+
+        def fetch(c):
+            if c % 2 == 0:
+                x12[c] = keep.tile([P, PACK, CHUNK], F32, name="x12", tag="after_products0", align_bytes=64)
+                x13[c] = keep.tile([P, PACK, CHUNK], F32, name="x13", tag="after_products1", align_bytes=64)
+            else:
+                both = keep.tile([P, 2, PACK, CHUNK], F32, name="x12_x13", tag="y%d" % last)
+                x12[c], x13[c] = both[:, 0], both[:, 1]
+            for t in ORDER[:-1]:
+                nc.scalar.activation(x12[c][:, t, :], up1[:, t, :].indirect(entries(lists["p2"], c * CHUNK, CHUNK)), ACT.Copy)
+            for t in ORDER:
+                nc.scalar.activation(x13[c][:, t, :], up1[:, t, :].indirect(entries(lists["p3"], c * CHUNK, CHUNK)), ACT.Copy)
+
+        def decay2(c):
+            dec2[c] = ring.tile([P, PACK, CHUNK], F32, name="dec2")
+            h, within = divmod(c * CHUNK, HALF)
+            nc.vector.tensor_tensor(dec2[c][:], dec[:, :, chunk(c)], ap[h][:, :, within : within + CHUNK], ALU.mult)
+
+        def grand_product_fused(c):
+            m2[c] = ring.tile([P, PACK, CHUNK], F32, name="m2")
+            picks = entries(lists["p2"], c * CHUNK, CHUNK)
+            nc.vector.tensor_tensor(m2[c][:, 0, :], up1_flat[:].indirect(picks), dec2[c][:, 0, :], ALU.mult)
+
+        def grand_product(c):
+            nc.vector.tensor_tensor(m2[c][:, 1:, :], x12[c][:, 1:, :], dec2[c][:, 1:, :], ALU.mult)
+
+        def second_sum(c):
+            up2[c] = ring.tile([P, PACK, CHUNK], F32, name="up2")
+            nc.vector.tensor_tensor(up2[c][:], m2[c][:], up1[:, :, chunk(c)], ALU.add)
+
+        def compare(c):
+            top[c] = ring.tile([P, CHUNK * PACK], BF16, name="top")
+            nc.vector.tensor_tensor(woven(top[c][:]), planes(up2[c][:]), planes(x13[c][:]), ALU.max)
+
+        def apply_sign(c):
+            hid[c] = ring.tile([P, CHUNK * PACK], BF16, name="hid", align_bytes=64)
+            nc.vector.tensor_tensor(hid[c][:], top[c][:], unit_sign[:].rearrange("p c t -> p (c t)"), ALU.mult)
+
+        def last_product(c):
             hid_words = ring.tile([P, CHUNK], U32, name="hid_words", align_bytes=64)
             hid_scales = ring.tile([P, CHUNK], U8, name="hid_scales", align_bytes=64)
-            nc.vector.tensor_tensor(dec2[:], dec[:, :, cols], ap[:, :, cols], ALU.mult)
-            nc.vector.tensor_tensor(m2[:], dec2[:], x12[:], ALU.mult)
-            nc.vector.tensor_tensor(up2[:], m2[:], up1[:, :, cols], ALU.add)
-            nc.vector.tensor_tensor(woven(top[:]), planes(up2[:]), planes(x13[:]), ALU.max)
-            nc.vector.tensor_tensor(hid[:], top[:], unit_sign[:].rearrange("p c t -> p (c t)"), ALU.mult)
-            nc.vector.quantize_mx(out=hid_words[:].bitcast(FP8X4), scales=hid_scales[:], in_=hid[:])
+            nc.vector.quantize_mx(out=hid_words[:].bitcast(FP8X4), scales=hid_scales[:], in_=hid[c][:])
             bank = psum.tile([P, PACK, CHUNK], F32, name="bank")
             for t in range(PACK):
                 nc.tensor.matmul_mx(
                     out=bank[:, t, :],
-                    lhsT=w3[2][:, 0, t, :].bitcast(FP4X4),
-                    lhsT_scale=w3[3][:, 0, t, :],
+                    lhsT=w3_dealt_words[:, t, :].bitcast(FP4X4),
+                    lhsT_scale=w3_dealt_scales[:, t, :],
                     rhs=hid_words[:].bitcast(FP8X4),
                     rhs_scale=hid_scales[:],
                     start=True,
                     stop=True,
                 )
-            result = keep.tile([P, PACK, CHUNK], F32, name="result%d" % c)
-            nc.scalar.activation(result[:], bank[:], ACT.Copy)
-            nc.sync.dma_start(out=out_rows[:, :, cols], in_=result[:])
-            results[c] = result
+            results[c] = keep.tile([P, PACK, CHUNK], F32, name="result%d" % c)
+            nc.scalar.activation(results[c][:], bank[:], ACT.Copy)
+            nc.sync.dma_start(out=out_rows[:, :, chunk(c)], in_=results[c][:])
+
+        def round_result(c):
+            rounded[c] = ring.tile([P, CHUNK * PACK], BF16, name="rounded", align_bytes=64)
+            nc.vector.tensor_copy(out=woven(rounded[c][:]), in_=planes(results[c][:]))
 
         def hand_on(c):
-            cols = slice(c * CHUNK, (c + 1) * CHUNK)
-            rounded = ring.tile([P, CHUNK * PACK], BF16, name="rounded", align_bytes=64)
-            nc.vector.tensor_copy(out=woven(rounded[:]), in_=planes(results[c][:]))
-            nc.vector.quantize_mx(out=out_words[:, cols].bitcast(FP8X4), scales=out_scales[:, cols], in_=rounded[:])
+            cols = chunk(c)
+            nc.vector.quantize_mx(out=out_words[:, cols].bitcast(FP8X4), scales=out_scales[:, cols], in_=rounded[c][:])
             nc.sync.dma_start(
                 out=out_1[0].rearrange("p c r -> p (c r)").bitcast(I32)[:, cols], in_=out_words[:, cols]
             )
 
-        lag = 2
-        for c in range(CHUNKS + lag):
+        for o in range(PASSES):
+            pick_scales(o)
+        pick_words(0)
+        for w in range(2):
+            deal(w, slice(first, first + 1))
+            product_pass(first, w, 0)
+        pick_words(1)
+        for w in range(2):
+            product_pass(first, w, 1)
+        leave_psum(first)
+        for ts in (slice(2, 4), slice(0, 1)):
+            for w in range(2):
+                deal(w, ts)
+            for t in range(ts.start, ts.stop):
+                for w in range(2):
+                    for o in range(PASSES):
+                        product_pass(t, w, o)
+                leave_psum(t)
+        deal_w3()
+        for n, t in enumerate(ORDER):
+            parent_decay(t, 0)
+            parent_product(t, 0)
+            if n > 0:
+                first_sum(ORDER[n - 1])
+            parent_product(t, 1)
+        decay2(0)
+        first_sum(last)
+        fetch(0)
+        fetch(1)
+        ap[1] = keep.tile([P, PACK, HALF], F32, name="ap1", tag="m1_%d" % last)
+        for t in ORDER:
+            parent_decay(t, 1)
+        grand_product_fused(0)
+        grand_product(0)
+        for c in range(CHUNKS + 2):
+            ahead, behind = c + 1, c - 2
             if c < CHUNKS:
-                hidden(c)
-            if c >= lag:
-                hand_on(c - lag)
+                second_sum(c)
+            if ahead < CHUNKS:
+                decay2(ahead)
+            if c < CHUNKS:
+                compare(c)
+            if c + 2 < CHUNKS:
+                fetch(c + 2)
+            if ahead < CHUNKS:
+                grand_product_fused(ahead)
+            if behind >= 0:
+                round_result(behind)
+            if c < CHUNKS:
+                apply_sign(c)
+            if ahead < CHUNKS:
+                grand_product(ahead)
+            if behind >= 0:
+                hand_on(behind)
+            if c < CHUNKS:
+                last_product(c)
         for q in range(4):
             queue = nc.sync if q % 2 == 0 else nc.scalar
             queue.dma_start(

@@ -22,8 +22,8 @@ PASSES = K // (P * PACK)
 HALF = S // 2
 CHUNK = 128
 CHUNKS = S // CHUNK
-RUN = 4
-ORDER = (1, 2, 3, 0)
+RUN = 2
+ORDER = (3, 2, 1, 0)
 
 
 def entries(lst, start, count):
@@ -60,12 +60,11 @@ def tile_picked_yptrjmp_max_po_kernel(
         for name in ("offs", "p1", "p2", "p3"):
             lists[name] = keep.tile([P, S // 16], U16, name="list_" + name)
 
-        raw_words = [keep.tile([P, PASSES, 2 * N], U8, name="raw_words%d" % w) for w in range(2)]
-        raw_scales = [keep.tile([P, PASSES, N], U8, name="raw_scales%d" % w) for w in range(2)]
+        raw_words = keep.tile([P, 2 * PASSES, 2 * N], U8, name="raw_words")
+        raw_scales = keep.tile([P, 2 * PASSES, N], U8, name="raw_scales")
         raw3_words = keep.tile([P, 1, 2 * N], U8, name="raw3_words")
-        raw3_scales = keep.tile([P, 1, N], U8, name="raw3_scales")
         table_words = [keep.tile([P, T], I32, name="table_words%d" % o) for o in range(PASSES)]
-        table_scales = keep.tile([P, PASSES, T], U8, name="table_scales")
+        table_scales = keep.tile([P, T], U8, name="table_scales", tag="scale_rows")
 
         def load_words(tile, words):
             nc.sync.dma_start(out=tile.bitcast(I32), in_=words.rearrange("o p b -> p o b").bitcast(I32))
@@ -74,64 +73,68 @@ def tile_picked_yptrjmp_max_po_kernel(
             nc.sync.dma_start(out=table_words[o][:], in_=x_words[o].rearrange("p c r -> p (c r)").bitcast(I32))
 
         nc.vector.memset(table_scales[:].bitcast(I32), 0)
-        for w in range(2):
-            nc.vector.memset(raw_scales[w][:].bitcast(I32), 0)
-        nc.vector.memset(raw3_scales[:].bitcast(I32), 0)
+        nc.vector.memset(raw_scales[:].bitcast(I32), 0)
         nc.sync.dma_start(lists["offs"][:], offs)
-        load_scales(nc, table_scales[:], x_scales)
+        for q in range(4):
+            nc.sync.dma_start(
+                out=table_scales[32 * q : 32 * q + 4 * PASSES, :].bitcast(I32),
+                in_=x_scales[:, 4 * q : 4 * q + 4, :].bitcast(I32),
+            )
         load_table_words(0)
-        load_words(raw_words[0][:], w2_words)
+        load_words(raw_words[:, :PASSES], w2_words)
+        load_scales(nc, raw_scales[:, :PASSES], w2_scales)
         load_table_words(1)
-        load_scales(nc, raw_scales[0][:], w2_scales)
-        load_words(raw_words[1][:], w1_words)
-        load_scales(nc, raw_scales[1][:], w1_scales)
+        load_words(raw_words[:, PASSES:], w1_words)
+        load_scales(nc, raw_scales[:, PASSES:], w1_scales)
         unit_sb = keep.tile([P, PACK], F32, name="unit_sb")
         nc.sync.dma_start(out=unit_sb[:], in_=unit.rearrange("(p t) o -> p (t o)", t=PACK))
         nc.sync.dma_start(lists["p1"][:], p1)
         load_words(raw3_words[:], w3_words)
-        load_scales(nc, raw3_scales[:], w3_scales)
         nc.sync.dma_start(lists["p2"][:], p2)
         nc.sync.dma_start(lists["p3"][:], p3)
 
         unit_abs = keep.tile([P, PACK], F32, name="unit_abs")
-        unit_sign = keep.tile([P, CHUNK, PACK], BF16, name="unit_sign")
+        unit_sign = keep.tile([P, PACK], BF16, name="unit_sign")
         twice_positive = keep.tile([P, PACK], F32, name="twice_positive")
-        nc.gpsimd.tensor_scalar(twice_positive[:], unit_sb[:], 0.0, 2.0, ALU.is_ge, ALU.mult)
-        nc.gpsimd.tensor_scalar(
-            unit_sign[:], twice_positive[:].unsqueeze(1).to_broadcast([P, CHUNK, PACK]), 1.0, -1.0, ALU.mult, ALU.add
-        )
-        nc.gpsimd.tensor_tensor(unit_abs[:], unit_sb[:], unit_sign[:, 0, :], ALU.mult)
+        nc.vector.tensor_scalar(twice_positive[:], unit_sb[:], 0.0, 2.0, ALU.is_ge, ALU.mult)
+        nc.vector.scalar_tensor_tensor(unit_abs[:], unit_sb[:], -1.0, unit_sb[:], ALU.mult, ALU.max)
+        nc.vector.tensor_scalar(unit_sign[:], twice_positive[:], 1.0, -1.0, ALU.mult, ALU.add)
 
         picked_words = [keep.tile([P, S], U32, name="picked_words%d" % o, tag="after_products%d" % o, align_bytes=64) for o in range(PASSES)]
         picked_scales = [keep.tile([P, S], U8, name="picked_scales%d" % o, align_bytes=64) for o in range(PASSES)]
         y = [keep.tile([P, S], F32, name="y%d" % t, tag="y%d" % t) for t in range(PACK)]
         m1 = [keep.tile([P, S], F32, name="m1_%d" % t, tag="m1_%d" % t) for t in range(PACK)]
-        dec = keep.tile([P, PACK, S], F32, name="dec")
+        dec_flat = keep.tile([P, PACK * S], F32, name="dec")
+        dec = dec_flat[:].rearrange("p (t j) -> p t j", t=PACK)
         ap = {0: keep.tile([P, PACK, HALF], F32, name="ap0")}
         up1_flat = keep.tile([P, PACK * S], F32, name="up1")
         up1 = up1_flat[:].rearrange("p (t j) -> p t j", t=PACK)
         dealt = {}
 
-        def deal(w, ts):
-            name = "%d_%d" % (w, ts.start)
-            count = ts.stop - ts.start
-            words = keep.tile([P, count, PASSES, 2 * P], U8, name="dealt_words" + name, align_bytes=64)
-            scales = keep.tile([P, count, PASSES, P], U8, name="dealt_scales" + name, align_bytes=64)
+        def deal(ws, ts):
+            name = "%d_%d" % (ws.start, ts.start)
+            gs = slice(ws.start * PASSES, ws.stop * PASSES)
+            shape = [P, gs.stop - gs.start, ts.stop - ts.start]
+            words = keep.tile(shape + [2 * P], U8, name="dealt_words" + name, align_bytes=64)
+            scales = keep.tile(shape + [P], U8, name="dealt_scales" + name, align_bytes=64)
             nc.vector.tensor_copy(
-                out=words[:].bitcast(U16).rearrange("p t o m -> p o t m"),
-                in_=raw_words[w][:].bitcast(U16).rearrange("p o (m t) -> p o t m", t=PACK)[:, :, ts, :],
+                out=words[:].bitcast(U16),
+                in_=raw_words[:].bitcast(U16).rearrange("p g (m t) -> p g t m", t=PACK)[:, gs, ts, :],
             )
             nc.vector.tensor_copy(
-                out=scales[:].rearrange("p t o m -> p o t m"),
-                in_=raw_scales[w][:].rearrange("p o (m t) -> p o t m", t=PACK)[:, :, ts, :],
+                out=scales[:], in_=raw_scales[:].rearrange("p g (m t) -> p g t m", t=PACK)[:, gs, ts, :]
             )
-            for t in range(ts.start, ts.stop):
-                dealt[t, w] = (words[:, t - ts.start], scales[:, t - ts.start])
+            for g in range(gs.start, gs.stop):
+                for t in range(ts.start, ts.stop):
+                    dealt[g, t] = (words[:, g - gs.start, t - ts.start, :], scales[:, g - gs.start, t - ts.start, :])
 
         w3_dealt_words = keep.tile([P, PACK, 2 * P], U8, name="w3_dealt_words", align_bytes=64)
         w3_dealt_scales = keep.tile([P, PACK, P], U8, name="w3_dealt_scales", align_bytes=64)
 
         def deal_w3():
+            raw3_scales = keep.tile([P, 1, N], U8, name="raw3_scales", tag="scale_rows")
+            nc.gpsimd.memset(raw3_scales[:].bitcast(I32), 0)
+            load_scales(nc, raw3_scales[:], w3_scales)
             nc.vector.tensor_copy(
                 out=w3_dealt_words[:].bitcast(U16),
                 in_=raw3_words[:, 0, :].bitcast(U16).rearrange("p (m t) -> p t m", t=PACK),
@@ -143,28 +146,37 @@ def tile_picked_yptrjmp_max_po_kernel(
         def pick_words(o):
             nc.vector.tensor_copy(picked_words[o][:], table_words[o][:].bitcast(U32).indirect(lists["offs"][:]))
 
-        def pick_scales(o):
-            nc.vector.tensor_copy(picked_scales[o][:], table_scales[:, o, :].indirect(lists["offs"][:]))
+        def pick_scales():
+            nc.vector.memset(picked_scales[1][:].bitcast(I32), 0)
+            nc.vector.tensor_copy(picked_scales[0][:], table_scales[:].indirect(lists["offs"][:]))
+            for q in range(4):
+                nc.sync.dma_start(
+                    out=picked_scales[1][32 * q : 32 * q + 4, :].bitcast(I32),
+                    in_=picked_scales[0][32 * q + 4 : 32 * q + 8, :].bitcast(I32),
+                )
 
         banks = {}
 
-        def product_pass(t, w, o):
-            words, scales = dealt[t, w]
-            if o == 0:
+        def product_pass(t, w, o, opens):
+            words, scales = dealt[w * PASSES + o, t]
+            if opens:
                 banks[t, w] = psum.tile([P, S], F32, name="bank")
             nc.tensor.matmul_mx(
                 out=banks[t, w][:],
-                lhsT=words[:, o, :].bitcast(FP4X4),
-                lhsT_scale=scales[:, o, :],
+                lhsT=words.bitcast(FP4X4),
+                lhsT_scale=scales,
                 rhs=picked_words[o][:].bitcast(FP8X4),
                 rhs_scale=picked_scales[o][:],
-                start=(o == 0),
-                stop=(o == PASSES - 1),
+                start=opens,
+                stop=not opens,
             )
 
         def leave_psum(t):
             nc.scalar.activation(dec[:, t, :], banks[t, 0][:], ACT.Sigmoid)
-            nc.scalar.activation(y[t][:], banks[t, 1][:], ACT.Copy, scale=unit_abs[:, t : t + 1])
+            if t == ORDER[0]:
+                nc.vector.tensor_scalar(y[t][:], banks[t, 1][:], unit_abs[:, t : t + 1], None, ALU.mult)
+            else:
+                nc.scalar.activation(y[t][:], banks[t, 1][:], ACT.Copy, scale=unit_abs[:, t : t + 1])
 
         def parent_product(t, h):
             cols = slice(h * HALF, (h + 1) * HALF)
@@ -187,6 +199,9 @@ def tile_picked_yptrjmp_max_po_kernel(
         def chunk(c):
             return slice(c * CHUNK, (c + 1) * CHUNK)
 
+        def half(h):
+            return slice(h * HALF, (h + 1) * HALF)
+
         def fetch(c):
             if c % 2 == 0:
                 x12[c] = keep.tile([P, PACK, CHUNK], F32, name="x12", tag="after_products0", align_bytes=64)
@@ -196,25 +211,33 @@ def tile_picked_yptrjmp_max_po_kernel(
                 x12[c], x13[c] = both[:, 0], both[:, 1]
             for t in ORDER[:-1]:
                 nc.scalar.activation(x12[c][:, t, :], up1[:, t, :].indirect(entries(lists["p2"], c * CHUNK, CHUNK)), ACT.Copy)
-            for t in ORDER:
+            for t in ORDER if c < CHUNKS - 1 else ORDER[:-1]:
                 nc.scalar.activation(x13[c][:, t, :], up1[:, t, :].indirect(entries(lists["p3"], c * CHUNK, CHUNK)), ACT.Copy)
 
-        def decay2(c):
-            dec2[c] = ring.tile([P, PACK, CHUNK], F32, name="dec2")
-            h, within = divmod(c * CHUNK, HALF)
-            nc.vector.tensor_tensor(dec2[c][:], dec[:, :, chunk(c)], ap[h][:, :, within : within + CHUNK], ALU.mult)
+        def fetch_last_on_vector():
+            c = CHUNKS - 1
+            nc.vector.tensor_copy(x13[c][:, last, :], up1[:, last, :].indirect(entries(lists["p3"], c * CHUNK, CHUNK)))
 
-        def grand_product_fused(c):
-            m2[c] = ring.tile([P, PACK, CHUNK], F32, name="m2")
-            picks = entries(lists["p2"], c * CHUNK, CHUNK)
-            nc.vector.tensor_tensor(m2[c][:, 0, :], up1_flat[:].indirect(picks), dec2[c][:, 0, :], ALU.mult)
+        def decay2(h):
+            dec2[h] = ring.tile([P, PACK, HALF], F32, name="dec2")
+            nc.vector.tensor_tensor(dec2[h][:, 1:, :], dec[:, 1:, half(h)], ap[h][:, 1:, :], ALU.mult)
+
+        def fused_grandparent(h):
+            picks = entries(lists["p2"], h * HALF, HALF)
+            nc.vector.tensor_tensor(dec2[h][:, 0, :], up1_flat[:].indirect(picks), dec[:, 0, half(h)], ALU.mult)
+
+        def fused_decay(h):
+            m2[h] = ring.tile([P, PACK, HALF], F32, name="m2")
+            picks = entries(lists["p1"], h * HALF, HALF)
+            nc.vector.tensor_tensor(m2[h][:, 0, :], dec_flat[:].indirect(picks), dec2[h][:, 0, :], ALU.mult)
 
         def grand_product(c):
-            nc.vector.tensor_tensor(m2[c][:, 1:, :], x12[c][:, 1:, :], dec2[c][:, 1:, :], ALU.mult)
+            h, cols = c // 2, chunk(c % 2)
+            nc.vector.tensor_tensor(m2[h][:, 1:, cols], x12[c][:, 1:, :], dec2[h][:, 1:, cols], ALU.mult)
 
         def second_sum(c):
             up2[c] = ring.tile([P, PACK, CHUNK], F32, name="up2")
-            nc.vector.tensor_tensor(up2[c][:], m2[c][:], up1[:, :, chunk(c)], ALU.add)
+            nc.vector.tensor_tensor(up2[c][:], m2[c // 2][:, :, chunk(c % 2)], up1[:, :, chunk(c)], ALU.add)
 
         def compare(c):
             top[c] = ring.tile([P, CHUNK * PACK], BF16, name="top")
@@ -222,25 +245,35 @@ def tile_picked_yptrjmp_max_po_kernel(
 
         def apply_sign(c):
             hid[c] = ring.tile([P, CHUNK * PACK], BF16, name="hid", align_bytes=64)
-            nc.vector.tensor_tensor(hid[c][:], top[c][:], unit_sign[:].rearrange("p c t -> p (c t)"), ALU.mult)
+            nc.vector.tensor_tensor(
+                hid[c][:].rearrange("p (j t) -> p j t", t=PACK),
+                top[c][:].rearrange("p (j t) -> p j t", t=PACK),
+                unit_sign[:].unsqueeze(1).to_broadcast([P, CHUNK, PACK]),
+                ALU.mult,
+            )
 
         def last_product(c):
             hid_words = ring.tile([P, CHUNK], U32, name="hid_words", align_bytes=64)
             hid_scales = ring.tile([P, CHUNK], U8, name="hid_scales", align_bytes=64)
             nc.vector.quantize_mx(out=hid_words[:].bitcast(FP8X4), scales=hid_scales[:], in_=hid[c][:])
-            bank = psum.tile([P, PACK, CHUNK], F32, name="bank")
-            for t in range(PACK):
-                nc.tensor.matmul_mx(
-                    out=bank[:, t, :],
-                    lhsT=w3_dealt_words[:, t, :].bitcast(FP4X4),
-                    lhsT_scale=w3_dealt_scales[:, t, :],
-                    rhs=hid_words[:].bitcast(FP8X4),
-                    rhs_scale=hid_scales[:],
-                    start=True,
-                    stop=True,
-                )
             results[c] = keep.tile([P, PACK, CHUNK], F32, name="result%d" % c)
-            nc.scalar.activation(results[c][:], bank[:], ACT.Copy)
+            group = PACK if c < CHUNKS - 1 else PACK // 2
+            for t0 in range(0, PACK, group):
+                bank = psum.tile([P, group, CHUNK], F32, name="bank")
+                for t in range(t0, t0 + group):
+                    nc.tensor.matmul_mx(
+                        out=bank[:, t - t0, :],
+                        lhsT=w3_dealt_words[:, t, :].bitcast(FP4X4),
+                        lhsT_scale=w3_dealt_scales[:, t, :],
+                        rhs=hid_words[:].bitcast(FP8X4),
+                        rhs_scale=hid_scales[:],
+                        start=True,
+                        stop=True,
+                    )
+                if t0 == 0:
+                    nc.scalar.activation(results[c][:, t0 : t0 + group, :], bank[:], ACT.Copy)
+                else:
+                    nc.vector.tensor_copy(results[c][:, t0 : t0 + group, :], bank[:])
             nc.sync.dma_start(out=out_rows[:, :, chunk(c)], in_=results[c][:])
 
         def round_result(c):
@@ -254,27 +287,27 @@ def tile_picked_yptrjmp_max_po_kernel(
                 out=out_1[0].rearrange("p c r -> p (c r)").bitcast(I32)[:, cols], in_=out_words[:, cols]
             )
 
-        for o in range(PASSES):
-            pick_scales(o)
+        pick_scales()
         pick_words(0)
-        for w in range(2):
-            deal(w, slice(first, first + 1))
-            product_pass(first, w, 0)
+        deal(slice(0, 1), slice(first, first + 1))
+        product_pass(first, 0, 0, True)
         pick_words(1)
+        deal(slice(1, 2), slice(first, first + 1))
+        product_pass(first, 1, 0, True)
         for w in range(2):
-            product_pass(first, w, 1)
+            product_pass(first, w, 1, False)
+        deal(slice(0, 2), slice(2, 3))
+        deal(slice(0, 2), slice(0, 2))
         leave_psum(first)
-        for ts in (slice(2, 4), slice(0, 1)):
+        for t in ORDER[1:]:
             for w in range(2):
-                deal(w, ts)
-            for t in range(ts.start, ts.stop):
-                for w in range(2):
-                    for o in range(PASSES):
-                        product_pass(t, w, o)
-                leave_psum(t)
+                product_pass(t, w, 1, True)
+                product_pass(t, w, 0, False)
+            leave_psum(t)
         deal_w3()
         for n, t in enumerate(ORDER):
-            parent_decay(t, 0)
+            if t != last:
+                parent_decay(t, 0)
             parent_product(t, 0)
             if n > 0:
                 first_sum(ORDER[n - 1])
@@ -284,32 +317,40 @@ def tile_picked_yptrjmp_max_po_kernel(
         fetch(0)
         fetch(1)
         ap[1] = keep.tile([P, PACK, HALF], F32, name="ap1", tag="m1_%d" % last)
-        for t in ORDER:
+        for t in ORDER[:-1]:
             parent_decay(t, 1)
-        grand_product_fused(0)
+        fused_grandparent(0)
+        fused_decay(0)
         grand_product(0)
         for c in range(CHUNKS + 2):
             ahead, behind = c + 1, c - 2
             if c < CHUNKS:
                 second_sum(c)
-            if ahead < CHUNKS:
-                decay2(ahead)
+            if c == 0:
+                grand_product(1)
+            if c == 1:
+                decay2(1)
+            if c == 2:
+                fetch_last_on_vector()
+                grand_product(3)
             if c < CHUNKS:
                 compare(c)
             if c + 2 < CHUNKS:
                 fetch(c + 2)
-            if ahead < CHUNKS:
-                grand_product_fused(ahead)
+            if c == 1:
+                fused_grandparent(1)
             if behind >= 0:
                 round_result(behind)
             if c < CHUNKS:
                 apply_sign(c)
-            if ahead < CHUNKS:
-                grand_product(ahead)
+            if c == 1:
+                fused_decay(1)
             if behind >= 0:
                 hand_on(behind)
             if c < CHUNKS:
                 last_product(c)
+            if c == 1:
+                grand_product(2)
         for q in range(4):
             queue = nc.sync if q % 2 == 0 else nc.scalar
             queue.dma_start(

@@ -19,30 +19,41 @@ ACT = mybir.ActivationFunctionType
 P = 128
 PACK = 4
 PASSES = K // (P * PACK)
+QUADRANTS = 4
+PER_COLUMN = 16
 HALF = S // 2
-CHUNK = 128
-CHUNKS = S // CHUNK
 RUN = 2
 ORDER = (3, 2, 1, 0)
+FIRST, LAST = ORDER[0], ORDER[-1]
+PIECES = (slice(0, 256), slice(256, 384), slice(384, 512))
+W2, W1 = 0, 1
 
 
-def entries(lst, start, count):
-    return lst[:, start // 16 : (start + count) // 16]
+def half(h):
+    return slice(h * HALF, (h + 1) * HALF)
+
+
+def entries(lst, cols):
+    return lst[:, cols.start // PER_COLUMN : cols.stop // PER_COLUMN]
+
+
+def load_words(nc, tile, words):
+    nc.sync.dma_start(out=tile.bitcast(I32), in_=words.rearrange("o p b -> p o b").bitcast(I32))
 
 
 def load_scales(nc, tile, scales):
-    for q in range(4):
+    for q in range(QUADRANTS):
         nc.sync.dma_start(
             out=tile[32 * q : 32 * q + 4].bitcast(I32),
             in_=scales[:, 4 * q : 4 * q + 4, :].rearrange("o r n -> r o n").bitcast(I32),
         )
 
 
-def woven(tile):
-    return tile.rearrange("p (c i t) -> p c t i", i=RUN, t=PACK)
+def side_by_side(ap):
+    return ap.rearrange("p (c i t) -> p c t i", i=RUN, t=PACK)
 
 
-def planes(ap):
+def in_runs(ap):
     return ap.rearrange("p t (c i) -> p c t i", i=RUN)
 
 
@@ -53,21 +64,17 @@ def tile_picked_yptrjmp_max_po_kernel(
     nc = tc.nc
     with ExitStack() as ctx:
         keep = ctx.enter_context(tc.tile_pool(name="keep", bufs=1))
-        ring = ctx.enter_context(tc.tile_pool(name="ring", bufs=2))
         psum = ctx.enter_context(tc.psum_pool(name="psum", bufs=8))
 
         lists = {}
         for name in ("offs", "p1", "p2", "p3"):
-            lists[name] = keep.tile([P, S // 16], U16, name="list_" + name)
-
+            lists[name] = keep.tile([P, S // PER_COLUMN], U16, name="list_" + name)
         raw_words = keep.tile([P, 2 * PASSES, 2 * N], U8, name="raw_words")
         raw_scales = keep.tile([P, 2 * PASSES, N], U8, name="raw_scales")
         raw3_words = keep.tile([P, 1, 2 * N], U8, name="raw3_words")
         table_words = [keep.tile([P, T], I32, name="table_words%d" % o) for o in range(PASSES)]
         table_scales = keep.tile([P, T], U8, name="table_scales", tag="scale_rows")
-
-        def load_words(tile, words):
-            nc.sync.dma_start(out=tile.bitcast(I32), in_=words.rearrange("o p b -> p o b").bitcast(I32))
+        unit_sb = keep.tile([P, PACK], F32, name="unit_sb")
 
         def load_table_words(o):
             nc.sync.dma_start(out=table_words[o][:], in_=x_words[o].rearrange("p c r -> p (c r)").bitcast(I32))
@@ -75,21 +82,20 @@ def tile_picked_yptrjmp_max_po_kernel(
         nc.vector.memset(table_scales[:].bitcast(I32), 0)
         nc.vector.memset(raw_scales[:].bitcast(I32), 0)
         nc.sync.dma_start(lists["offs"][:], offs)
-        for q in range(4):
+        for q in range(QUADRANTS):
             nc.sync.dma_start(
                 out=table_scales[32 * q : 32 * q + 4 * PASSES, :].bitcast(I32),
                 in_=x_scales[:, 4 * q : 4 * q + 4, :].bitcast(I32),
             )
         load_table_words(0)
-        load_words(raw_words[:, :PASSES], w2_words)
+        load_words(nc, raw_words[:, :PASSES], w2_words)
         load_scales(nc, raw_scales[:, :PASSES], w2_scales)
         load_table_words(1)
-        load_words(raw_words[:, PASSES:], w1_words)
+        load_words(nc, raw_words[:, PASSES:], w1_words)
         load_scales(nc, raw_scales[:, PASSES:], w1_scales)
-        unit_sb = keep.tile([P, PACK], F32, name="unit_sb")
         nc.sync.dma_start(out=unit_sb[:], in_=unit.rearrange("(p t) o -> p (t o)", t=PACK))
         nc.sync.dma_start(lists["p1"][:], p1)
-        load_words(raw3_words[:], w3_words)
+        load_words(nc, raw3_words[:], w3_words)
         nc.sync.dma_start(lists["p2"][:], p2)
         nc.sync.dma_start(lists["p3"][:], p3)
 
@@ -100,20 +106,36 @@ def tile_picked_yptrjmp_max_po_kernel(
         nc.vector.scalar_tensor_tensor(unit_abs[:], unit_sb[:], -1.0, unit_sb[:], ALU.mult, ALU.max)
         nc.vector.tensor_scalar(unit_sign[:], twice_positive[:], 1.0, -1.0, ALU.mult, ALU.add)
 
-        picked_words = [keep.tile([P, S], U32, name="picked_words%d" % o, tag="after_products%d" % o, align_bytes=64) for o in range(PASSES)]
+        picked_words = [
+            keep.tile([P, S], U32, name="picked_words%d" % o, tag="picked%d" % o, align_bytes=64)
+            for o in range(PASSES)
+        ]
         picked_scales = [keep.tile([P, S], U8, name="picked_scales%d" % o, align_bytes=64) for o in range(PASSES)]
         y = [keep.tile([P, S], F32, name="y%d" % t, tag="y%d" % t) for t in range(PACK)]
         m1 = [keep.tile([P, S], F32, name="m1_%d" % t, tag="m1_%d" % t) for t in range(PACK)]
-        dec_flat = keep.tile([P, PACK * S], F32, name="dec")
-        dec = dec_flat[:].rearrange("p (t j) -> p t j", t=PACK)
+        dec_whole = keep.tile([P, PACK * S], F32, name="dec")
+        dec = dec_whole[:].rearrange("p (t j) -> p t j", t=PACK)
         ap = {0: keep.tile([P, PACK, HALF], F32, name="ap0")}
-        up1_flat = keep.tile([P, PACK * S], F32, name="up1")
-        up1 = up1_flat[:].rearrange("p (t j) -> p t j", t=PACK)
-        dealt = {}
+        up1_whole = keep.tile([P, PACK * S], F32, name="up1")
+        up1 = up1_whole[:].rearrange("p (t j) -> p t j", t=PACK)
+        w3_dealt_words = keep.tile([P, PACK, 2 * P], U8, name="w3_dealt_words", align_bytes=64)
+        w3_dealt_scales = keep.tile([P, PACK, P], U8, name="w3_dealt_scales", align_bytes=64)
+        dealt, banks = {}, {}
 
-        def deal(ws, ts):
-            name = "%d_%d" % (ws.start, ts.start)
-            gs = slice(ws.start * PASSES, ws.stop * PASSES)
+        def pick_scales():
+            nc.vector.memset(picked_scales[1][:].bitcast(I32), 0)
+            nc.vector.tensor_copy(picked_scales[0][:], table_scales[:].indirect(lists["offs"][:]))
+            for q in range(QUADRANTS):
+                nc.sync.dma_start(
+                    out=picked_scales[1][32 * q : 32 * q + 4, :].bitcast(I32),
+                    in_=picked_scales[0][32 * q + 4 : 32 * q + 8, :].bitcast(I32),
+                )
+
+        def pick_words(o):
+            nc.vector.tensor_copy(picked_words[o][:], table_words[o][:].bitcast(U32).indirect(lists["offs"][:]))
+
+        def deal(gs, ts):
+            name = "%d_%d" % (gs.start, ts.start)
             shape = [P, gs.stop - gs.start, ts.stop - ts.start]
             words = keep.tile(shape + [2 * P], U8, name="dealt_words" + name, align_bytes=64)
             scales = keep.tile(shape + [P], U8, name="dealt_scales" + name, align_bytes=64)
@@ -128,9 +150,6 @@ def tile_picked_yptrjmp_max_po_kernel(
                 for t in range(ts.start, ts.stop):
                     dealt[g, t] = (words[:, g - gs.start, t - ts.start, :], scales[:, g - gs.start, t - ts.start, :])
 
-        w3_dealt_words = keep.tile([P, PACK, 2 * P], U8, name="w3_dealt_words", align_bytes=64)
-        w3_dealt_scales = keep.tile([P, PACK, P], U8, name="w3_dealt_scales", align_bytes=64)
-
         def deal_w3():
             raw3_scales = keep.tile([P, 1, N], U8, name="raw3_scales", tag="scale_rows")
             nc.gpsimd.memset(raw3_scales[:].bitcast(I32), 0)
@@ -142,20 +161,6 @@ def tile_picked_yptrjmp_max_po_kernel(
             nc.vector.tensor_copy(
                 out=w3_dealt_scales[:], in_=raw3_scales[:, 0, :].rearrange("p (m t) -> p t m", t=PACK)
             )
-
-        def pick_words(o):
-            nc.vector.tensor_copy(picked_words[o][:], table_words[o][:].bitcast(U32).indirect(lists["offs"][:]))
-
-        def pick_scales():
-            nc.vector.memset(picked_scales[1][:].bitcast(I32), 0)
-            nc.vector.tensor_copy(picked_scales[0][:], table_scales[:].indirect(lists["offs"][:]))
-            for q in range(4):
-                nc.sync.dma_start(
-                    out=picked_scales[1][32 * q : 32 * q + 4, :].bitcast(I32),
-                    in_=picked_scales[0][32 * q + 4 : 32 * q + 8, :].bitcast(I32),
-                )
-
-        banks = {}
 
         def product_pass(t, w, o, opens):
             words, scales = dealt[w * PASSES + o, t]
@@ -172,95 +177,101 @@ def tile_picked_yptrjmp_max_po_kernel(
             )
 
         def leave_psum(t):
-            nc.scalar.activation(dec[:, t, :], banks[t, 0][:], ACT.Sigmoid)
-            if t == ORDER[0]:
-                nc.vector.tensor_scalar(y[t][:], banks[t, 1][:], unit_abs[:, t : t + 1], None, ALU.mult)
+            nc.scalar.activation(dec[:, t, :], banks[t, W2][:], ACT.Sigmoid)
+            if t == FIRST:
+                nc.vector.tensor_scalar(y[t][:], banks[t, W1][:], unit_abs[:, t : t + 1], None, ALU.mult)
             else:
-                nc.scalar.activation(y[t][:], banks[t, 1][:], ACT.Copy, scale=unit_abs[:, t : t + 1])
+                nc.scalar.activation(y[t][:], banks[t, W1][:], ACT.Copy, scale=unit_abs[:, t : t + 1])
 
-        def parent_product(t, h):
-            cols = slice(h * HALF, (h + 1) * HALF)
-            picks = entries(lists["p1"], h * HALF, HALF)
-            nc.vector.tensor_tensor(m1[t][:, cols], y[t][:].indirect(picks), dec[:, t, cols], ALU.mult)
-
-        def parent_decay(t, h):
-            picks = entries(lists["p1"], h * HALF, HALF)
-            nc.scalar.activation(ap[h][:, t, :], dec[:, t, :].indirect(picks), ACT.Copy)
-
-        def first_sum(t):
-            nc.vector.tensor_tensor(up1[:, t, :], m1[t][:], y[t][:], ALU.add)
+        first_tile = slice(FIRST, FIRST + 1)
+        both_weights = slice(0, 2 * PASSES)
+        pick_scales()
+        pick_words(0)
+        deal(slice(0, PASSES), first_tile)
+        product_pass(FIRST, W2, 0, True)
+        pick_words(1)
+        deal(slice(PASSES, 2 * PASSES), first_tile)
+        product_pass(FIRST, W1, 0, True)
+        for w in (W2, W1):
+            product_pass(FIRST, w, 1, False)
+        deal(both_weights, slice(2, 3))
+        deal(both_weights, slice(0, 2))
+        leave_psum(FIRST)
+        for t in ORDER[1:]:
+            for w in (W2, W1):
+                product_pass(t, w, 1, True)
+                product_pass(t, w, 0, False)
+            leave_psum(t)
+        deal_w3()
 
         out_words = keep.tile([P, S], I32, name="out_words", align_bytes=64)
         out_scales = keep.tile([P, S], U8, name="out_scales", align_bytes=64)
         out_rows = out_0.rearrange("(p t) j -> p t j", t=PACK)
-        first, last = ORDER[0], ORDER[-1]
-        x12, x13, dec2, m2, up2, top, hid, results, rounded = {}, {}, {}, {}, {}, {}, {}, {}, {}
+        factor = [keep.tile([P, PACK, HALF], F32, name="factor%d" % h) for h in range(2)]
+        m2 = [keep.tile([P, PACK, HALF], F32, name="m2_%d" % h) for h in range(2)]
+        up2 = [keep.tile([P, PACK, HALF], F32, name="up2_%d" % h) for h in range(2)]
+        x12, x13 = {}, {}
+        top, hid, results, result_banks, rounded = {}, {}, {}, {}, {}
 
-        def chunk(c):
-            return slice(c * CHUNK, (c + 1) * CHUNK)
+        def parent_product(t, h):
+            picks = entries(lists["p1"], half(h))
+            nc.vector.tensor_tensor(m1[t][:, half(h)], y[t][:].indirect(picks), dec[:, t, half(h)], ALU.mult)
 
-        def half(h):
-            return slice(h * HALF, (h + 1) * HALF)
+        def first_sum(t):
+            nc.vector.tensor_tensor(up1[:, t, :], m1[t][:], y[t][:], ALU.add)
 
-        def fetch(c):
-            if c % 2 == 0:
-                x12[c] = keep.tile([P, PACK, CHUNK], F32, name="x12", tag="after_products0", align_bytes=64)
-                x13[c] = keep.tile([P, PACK, CHUNK], F32, name="x13", tag="after_products1", align_bytes=64)
-            else:
-                both = keep.tile([P, 2, PACK, CHUNK], F32, name="x12_x13", tag="y%d" % last)
-                x12[c], x13[c] = both[:, 0], both[:, 1]
-            for t in ORDER[:-1]:
-                nc.scalar.activation(x12[c][:, t, :], up1[:, t, :].indirect(entries(lists["p2"], c * CHUNK, CHUNK)), ACT.Copy)
-            for t in ORDER if c < CHUNKS - 1 else ORDER[:-1]:
-                nc.scalar.activation(x13[c][:, t, :], up1[:, t, :].indirect(entries(lists["p3"], c * CHUNK, CHUNK)), ACT.Copy)
+        def fetch(out, window, name, cols):
+            nc.scalar.activation(out, window.indirect(entries(lists[name], cols)), ACT.Copy)
 
-        def fetch_last_on_vector():
-            c = CHUNKS - 1
-            nc.vector.tensor_copy(x13[c][:, last, :], up1[:, last, :].indirect(entries(lists["p3"], c * CHUNK, CHUNK)))
+        def factor_tile0(h):
+            picks = entries(lists["p2"], half(h))
+            nc.vector.tensor_tensor(factor[h][:, 0, :], up1_whole[:].indirect(picks), dec[:, 0, half(h)], ALU.mult)
 
-        def decay2(h):
-            dec2[h] = ring.tile([P, PACK, HALF], F32, name="dec2")
-            nc.vector.tensor_tensor(dec2[h][:, 1:, :], dec[:, 1:, half(h)], ap[h][:, 1:, :], ALU.mult)
+        def factor_others(h):
+            nc.vector.tensor_tensor(factor[h][:, 1:, :], dec[:, 1:, half(h)], ap[h][:, 1:, :], ALU.mult)
 
-        def fused_grandparent(h):
-            picks = entries(lists["p2"], h * HALF, HALF)
-            nc.vector.tensor_tensor(dec2[h][:, 0, :], up1_flat[:].indirect(picks), dec[:, 0, half(h)], ALU.mult)
+        def m2_tile0(h):
+            picks = entries(lists["p1"], half(h))
+            nc.vector.tensor_tensor(m2[h][:, 0, :], dec_whole[:].indirect(picks), factor[h][:, 0, :], ALU.mult)
 
-        def fused_decay(h):
-            m2[h] = ring.tile([P, PACK, HALF], F32, name="m2")
-            picks = entries(lists["p1"], h * HALF, HALF)
-            nc.vector.tensor_tensor(m2[h][:, 0, :], dec_flat[:].indirect(picks), dec2[h][:, 0, :], ALU.mult)
+        def m2_others(h):
+            nc.vector.tensor_tensor(m2[h][:, 1:, :], x12[h][:, 1:, :], factor[h][:, 1:, :], ALU.mult)
 
-        def grand_product(c):
-            h, cols = c // 2, chunk(c % 2)
-            nc.vector.tensor_tensor(m2[h][:, 1:, cols], x12[c][:, 1:, :], dec2[h][:, 1:, cols], ALU.mult)
+        def second_sum(h):
+            nc.vector.tensor_tensor(up2[h][:], m2[h][:], up1[:, :, half(h)], ALU.add)
 
-        def second_sum(c):
-            up2[c] = ring.tile([P, PACK, CHUNK], F32, name="up2")
-            nc.vector.tensor_tensor(up2[c][:], m2[c // 2][:, :, chunk(c % 2)], up1[:, :, chunk(c)], ALU.add)
+        def in_half(c):
+            h = PIECES[c].start // HALF
+            return h, slice(PIECES[c].start - h * HALF, PIECES[c].stop - h * HALF)
+
+        def width(c):
+            return PIECES[c].stop - PIECES[c].start
 
         def compare(c):
-            top[c] = ring.tile([P, CHUNK * PACK], BF16, name="top")
-            nc.vector.tensor_tensor(woven(top[c][:]), planes(up2[c][:]), planes(x13[c][:]), ALU.max)
+            h, cols = in_half(c)
+            top[c] = keep.tile([P, width(c) * PACK], BF16, name="top%d" % c)
+            nc.vector.tensor_tensor(
+                side_by_side(top[c][:]), in_runs(up2[h][:, :, cols]), in_runs(x13[h][:, :, cols]), ALU.max
+            )
 
         def apply_sign(c):
-            hid[c] = ring.tile([P, CHUNK * PACK], BF16, name="hid", align_bytes=64)
+            hid[c] = keep.tile([P, width(c) * PACK], BF16, name="hid%d" % c, align_bytes=64)
             nc.vector.tensor_tensor(
                 hid[c][:].rearrange("p (j t) -> p j t", t=PACK),
                 top[c][:].rearrange("p (j t) -> p j t", t=PACK),
-                unit_sign[:].unsqueeze(1).to_broadcast([P, CHUNK, PACK]),
+                unit_sign[:].unsqueeze(1).to_broadcast([P, width(c), PACK]),
                 ALU.mult,
             )
 
-        def last_product(c):
-            hid_words = ring.tile([P, CHUNK], U32, name="hid_words", align_bytes=64)
-            hid_scales = ring.tile([P, CHUNK], U8, name="hid_scales", align_bytes=64)
+        def last_product(c, tiles_a_bank):
+            hid_words = keep.tile([P, width(c)], U32, name="hid_words%d" % c, align_bytes=64)
+            hid_scales = keep.tile([P, width(c)], U8, name="hid_scales%d" % c, align_bytes=64)
             nc.vector.quantize_mx(out=hid_words[:].bitcast(FP8X4), scales=hid_scales[:], in_=hid[c][:])
-            results[c] = keep.tile([P, PACK, CHUNK], F32, name="result%d" % c)
-            group = PACK if c < CHUNKS - 1 else PACK // 2
-            for t0 in range(0, PACK, group):
-                bank = psum.tile([P, group, CHUNK], F32, name="bank")
-                for t in range(t0, t0 + group):
+            results[c] = keep.tile([P, PACK, width(c)], F32, name="result%d" % c)
+            result_banks[c] = []
+            for t0 in range(0, PACK, tiles_a_bank):
+                bank = psum.tile([P, tiles_a_bank, width(c)], F32, name="bank")
+                for t in range(t0, t0 + tiles_a_bank):
                     nc.tensor.matmul_mx(
                         out=bank[:, t - t0, :],
                         lhsT=w3_dealt_words[:, t, :].bitcast(FP4X4),
@@ -270,88 +281,80 @@ def tile_picked_yptrjmp_max_po_kernel(
                         start=True,
                         stop=True,
                     )
-                if t0 == 0:
-                    nc.scalar.activation(results[c][:, t0 : t0 + group, :], bank[:], ACT.Copy)
+                result_banks[c].append((results[c][:, t0 : t0 + tiles_a_bank, :], bank))
+
+        def store_result(c):
+            for n, (rows, bank) in enumerate(result_banks[c]):
+                if c == len(PIECES) - 1 and n == 1:
+                    nc.vector.tensor_copy(rows, bank[:])
                 else:
-                    nc.vector.tensor_copy(results[c][:, t0 : t0 + group, :], bank[:])
-            nc.sync.dma_start(out=out_rows[:, :, chunk(c)], in_=results[c][:])
+                    nc.scalar.activation(rows, bank[:], ACT.Copy)
+            nc.sync.dma_start(out=out_rows[:, :, PIECES[c]], in_=results[c][:])
 
         def round_result(c):
-            rounded[c] = ring.tile([P, CHUNK * PACK], BF16, name="rounded", align_bytes=64)
-            nc.vector.tensor_copy(out=woven(rounded[c][:]), in_=planes(results[c][:]))
+            rounded[c] = keep.tile([P, width(c) * PACK], BF16, name="rounded%d" % c, align_bytes=64)
+            nc.vector.tensor_copy(out=side_by_side(rounded[c][:]), in_=in_runs(results[c][:]))
 
         def hand_on(c):
-            cols = chunk(c)
+            cols = PIECES[c]
             nc.vector.quantize_mx(out=out_words[:, cols].bitcast(FP8X4), scales=out_scales[:, cols], in_=rounded[c][:])
             nc.sync.dma_start(
                 out=out_1[0].rearrange("p c r -> p (c r)").bitcast(I32)[:, cols], in_=out_words[:, cols]
             )
 
-        pick_scales()
-        pick_words(0)
-        deal(slice(0, 1), slice(first, first + 1))
-        product_pass(first, 0, 0, True)
-        pick_words(1)
-        deal(slice(1, 2), slice(first, first + 1))
-        product_pass(first, 1, 0, True)
-        for w in range(2):
-            product_pass(first, w, 1, False)
-        deal(slice(0, 2), slice(2, 3))
-        deal(slice(0, 2), slice(0, 2))
-        leave_psum(first)
-        for t in ORDER[1:]:
-            for w in range(2):
-                product_pass(t, w, 1, True)
-                product_pass(t, w, 0, False)
-            leave_psum(t)
-        deal_w3()
         for n, t in enumerate(ORDER):
-            if t != last:
-                parent_decay(t, 0)
+            if t != LAST:
+                fetch(ap[0][:, t, :], dec[:, t, :], "p1", half(0))
             parent_product(t, 0)
             if n > 0:
                 first_sum(ORDER[n - 1])
             parent_product(t, 1)
-        decay2(0)
-        first_sum(last)
-        fetch(0)
-        fetch(1)
-        ap[1] = keep.tile([P, PACK, HALF], F32, name="ap1", tag="m1_%d" % last)
+        factor_others(0)
+        first_sum(LAST)
+
+        x12[0] = keep.tile([P, PACK, HALF], F32, name="x12_0", tag="picked0", align_bytes=64)
+        x13[0] = keep.tile([P, PACK, HALF], F32, name="x13_0", tag="picked1", align_bytes=64)
         for t in ORDER[:-1]:
-            parent_decay(t, 1)
-        fused_grandparent(0)
-        fused_decay(0)
-        grand_product(0)
-        for c in range(CHUNKS + 2):
-            ahead, behind = c + 1, c - 2
-            if c < CHUNKS:
-                second_sum(c)
-            if c == 0:
-                grand_product(1)
-            if c == 1:
-                decay2(1)
-            if c == 2:
-                fetch_last_on_vector()
-                grand_product(3)
-            if c < CHUNKS:
-                compare(c)
-            if c + 2 < CHUNKS:
-                fetch(c + 2)
-            if c == 1:
-                fused_grandparent(1)
-            if behind >= 0:
-                round_result(behind)
-            if c < CHUNKS:
-                apply_sign(c)
-            if c == 1:
-                fused_decay(1)
-            if behind >= 0:
-                hand_on(behind)
-            if c < CHUNKS:
-                last_product(c)
-            if c == 1:
-                grand_product(2)
-        for q in range(4):
+            fetch(x12[0][:, t, :], up1[:, t, :], "p2", half(0))
+        for t in ORDER:
+            fetch(x13[0][:, t, :], up1[:, t, :], "p3", half(0))
+        x12[1] = keep.tile([P, PACK, HALF], F32, name="x12_1", tag="y%d" % LAST)
+        ap_and_x13 = keep.tile([P, 2, PACK, HALF], F32, name="ap1_x13_1", tag="m1_%d" % LAST)
+        ap[1], x13[1] = ap_and_x13[:, 0], ap_and_x13[:, 1]
+        for t in ORDER[:-1]:
+            fetch(ap[1][:, t, :], dec[:, t, :], "p1", half(1))
+        for t in ORDER[:-1]:
+            fetch(x12[1][:, t, :], up1[:, t, :], "p2", half(1))
+        for c in (1, 2):
+            for t in ORDER:
+                fetch(x13[1][:, t, in_half(c)[1]], up1[:, t, :], "p3", PIECES[c])
+
+        factor_tile0(0)
+        m2_others(0)
+        m2_tile0(0)
+        factor_tile0(1)
+        second_sum(0)
+        m2_tile0(1)
+        compare(0)
+        factor_others(1)
+        apply_sign(0)
+        m2_others(1)
+        last_product(0, 2)
+        store_result(0)
+        second_sum(1)
+        for step in (compare, apply_sign):
+            step(1)
+            step(2)
+        last_product(1, PACK)
+        last_product(2, 2)
+        store_result(1)
+        round_result(0)
+        hand_on(0)
+        store_result(2)
+        for step in (round_result, hand_on):
+            step(1)
+            step(2)
+        for q in range(QUADRANTS):
             queue = nc.sync if q % 2 == 0 else nc.scalar
             queue.dma_start(
                 out=out_2[0, 4 * q : 4 * q + 4, :].bitcast(I32),

from contextlib import ExitStack

import concourse.mybir as mybir

K, T, S, N, H = 1024, 1024, 512, 512, 512
FLOPS = 2 * (2 * K * N * S) + 2 * H * N * S

F32 = mybir.dt.float32
BF16 = mybir.dt.bfloat16
I32 = mybir.dt.int32
U32 = mybir.dt.uint32
U16 = mybir.dt.uint16
U8 = mybir.dt.uint8
FP8X4 = mybir.dt.float8_e4m3fn_x4
FP4X4 = mybir.dt.float4_e2m1fn_x4
ALU = mybir.AluOpType
ACT = mybir.ActivationFunctionType

P = 128
PACK = 4
PASSES = K // (P * PACK)
QUADRANTS = 4
PER_COLUMN = 16
HALF = S // 2
RUN = 2
ORDER = (3, 2, 1, 0)
FIRST, LAST = ORDER[0], ORDER[-1]
PIECES = (slice(0, 256), slice(256, 384), slice(384, 512))
W2, W1 = 0, 1


def half(h):
    return slice(h * HALF, (h + 1) * HALF)


def entries(lst, cols):
    return lst[:, cols.start // PER_COLUMN : cols.stop // PER_COLUMN]


def load_words(nc, tile, words):
    nc.sync.dma_start(out=tile.bitcast(I32), in_=words.rearrange("o p b -> p o b").bitcast(I32))


def load_scales(nc, tile, scales):
    for q in range(QUADRANTS):
        nc.sync.dma_start(
            out=tile[32 * q : 32 * q + 4].bitcast(I32),
            in_=scales[:, 4 * q : 4 * q + 4, :].rearrange("o r n -> r o n").bitcast(I32),
        )


def side_by_side(ap):
    return ap.rearrange("p (c i t) -> p c t i", i=RUN, t=PACK)


def in_runs(ap):
    return ap.rearrange("p t (c i) -> p c t i", i=RUN)


def tile_picked_yptrjmp_max_po_kernel(
    tc, x_words, x_scales, w1_words, w1_scales, w2_words, w2_scales, unit, w3_words, w3_scales,
    offs, p1, p2, p3, out_0, out_1, out_2,
):
    nc = tc.nc
    with ExitStack() as ctx:
        keep = ctx.enter_context(tc.tile_pool(name="keep", bufs=1))
        psum = ctx.enter_context(tc.psum_pool(name="psum", bufs=8))

        lists = {}
        for name in ("offs", "p1", "p2", "p3"):
            lists[name] = keep.tile([P, S // PER_COLUMN], U16, name="list_" + name)
        raw_words = keep.tile([P, 2 * PASSES, 2 * N], U8, name="raw_words")
        raw_scales = keep.tile([P, 2 * PASSES, N], U8, name="raw_scales")
        raw3_words = keep.tile([P, 1, 2 * N], U8, name="raw3_words")
        table_words = [keep.tile([P, T], I32, name="table_words%d" % o) for o in range(PASSES)]
        table_scales = keep.tile([P, T], U8, name="table_scales", tag="scale_rows")
        unit_sb = keep.tile([P, PACK], F32, name="unit_sb")

        def load_table_words(o):
            nc.sync.dma_start(out=table_words[o][:], in_=x_words[o].rearrange("p c r -> p (c r)").bitcast(I32))

        nc.vector.memset(table_scales[:].bitcast(I32), 0)
        nc.vector.memset(raw_scales[:].bitcast(I32), 0)
        nc.sync.dma_start(lists["offs"][:], offs)
        for q in range(QUADRANTS):
            nc.sync.dma_start(
                out=table_scales[32 * q : 32 * q + 4 * PASSES, :].bitcast(I32),
                in_=x_scales[:, 4 * q : 4 * q + 4, :].bitcast(I32),
            )
        load_table_words(0)
        load_words(nc, raw_words[:, :PASSES], w2_words)
        load_scales(nc, raw_scales[:, :PASSES], w2_scales)
        load_table_words(1)
        load_words(nc, raw_words[:, PASSES:], w1_words)
        load_scales(nc, raw_scales[:, PASSES:], w1_scales)
        nc.sync.dma_start(out=unit_sb[:], in_=unit.rearrange("(p t) o -> p (t o)", t=PACK))
        nc.sync.dma_start(lists["p1"][:], p1)
        load_words(nc, raw3_words[:], w3_words)
        nc.sync.dma_start(lists["p2"][:], p2)
        nc.sync.dma_start(lists["p3"][:], p3)

        unit_abs = keep.tile([P, PACK], F32, name="unit_abs")
        unit_sign = keep.tile([P, PACK], BF16, name="unit_sign")
        twice_positive = keep.tile([P, PACK], F32, name="twice_positive")
        nc.vector.tensor_scalar(twice_positive[:], unit_sb[:], 0.0, 2.0, ALU.is_ge, ALU.mult)
        nc.vector.scalar_tensor_tensor(unit_abs[:], unit_sb[:], -1.0, unit_sb[:], ALU.mult, ALU.max)
        nc.vector.tensor_scalar(unit_sign[:], twice_positive[:], 1.0, -1.0, ALU.mult, ALU.add)

        picked_words = [
            keep.tile([P, S], U32, name="picked_words%d" % o, tag="picked%d" % o, align_bytes=64)
            for o in range(PASSES)
        ]
        picked_scales = [keep.tile([P, S], U8, name="picked_scales%d" % o, align_bytes=64) for o in range(PASSES)]
        y = [keep.tile([P, S], F32, name="y%d" % t, tag="y%d" % t) for t in range(PACK)]
        m1 = [keep.tile([P, S], F32, name="m1_%d" % t, tag="m1_%d" % t) for t in range(PACK)]
        dec_whole = keep.tile([P, PACK * S], F32, name="dec")
        dec = dec_whole[:].rearrange("p (t j) -> p t j", t=PACK)
        ap = {0: keep.tile([P, PACK, HALF], F32, name="ap0")}
        up1_whole = keep.tile([P, PACK * S], F32, name="up1")
        up1 = up1_whole[:].rearrange("p (t j) -> p t j", t=PACK)
        w3_dealt_words = keep.tile([P, PACK, 2 * P], U8, name="w3_dealt_words", align_bytes=64)
        w3_dealt_scales = keep.tile([P, PACK, P], U8, name="w3_dealt_scales", align_bytes=64)
        dealt, banks = {}, {}

        def pick_scales():
            nc.vector.memset(picked_scales[1][:].bitcast(I32), 0)
            nc.vector.tensor_copy(picked_scales[0][:], table_scales[:].indirect(lists["offs"][:]))
            for q in range(QUADRANTS):
                nc.sync.dma_start(
                    out=picked_scales[1][32 * q : 32 * q + 4, :].bitcast(I32),
                    in_=picked_scales[0][32 * q + 4 : 32 * q + 8, :].bitcast(I32),
                )

        def pick_words(o):
            nc.vector.tensor_copy(picked_words[o][:], table_words[o][:].bitcast(U32).indirect(lists["offs"][:]))

        def deal(gs, ts):
            name = "%d_%d" % (gs.start, ts.start)
            shape = [P, gs.stop - gs.start, ts.stop - ts.start]
            words = keep.tile(shape + [2 * P], U8, name="dealt_words" + name, align_bytes=64)
            scales = keep.tile(shape + [P], U8, name="dealt_scales" + name, align_bytes=64)
            nc.vector.tensor_copy(
                out=words[:].bitcast(U16),
                in_=raw_words[:].bitcast(U16).rearrange("p g (m t) -> p g t m", t=PACK)[:, gs, ts, :],
            )
            nc.vector.tensor_copy(
                out=scales[:], in_=raw_scales[:].rearrange("p g (m t) -> p g t m", t=PACK)[:, gs, ts, :]
            )
            for g in range(gs.start, gs.stop):
                for t in range(ts.start, ts.stop):
                    dealt[g, t] = (words[:, g - gs.start, t - ts.start, :], scales[:, g - gs.start, t - ts.start, :])

        def deal_w3():
            raw3_scales = keep.tile([P, 1, N], U8, name="raw3_scales", tag="scale_rows")
            nc.gpsimd.memset(raw3_scales[:].bitcast(I32), 0)
            load_scales(nc, raw3_scales[:], w3_scales)
            nc.vector.tensor_copy(
                out=w3_dealt_words[:].bitcast(U16),
                in_=raw3_words[:, 0, :].bitcast(U16).rearrange("p (m t) -> p t m", t=PACK),
            )
            nc.vector.tensor_copy(
                out=w3_dealt_scales[:], in_=raw3_scales[:, 0, :].rearrange("p (m t) -> p t m", t=PACK)
            )

        def product_pass(t, w, o, opens):
            words, scales = dealt[w * PASSES + o, t]
            if opens:
                banks[t, w] = psum.tile([P, S], F32, name="bank")
            nc.tensor.matmul_mx(
                out=banks[t, w][:],
                lhsT=words.bitcast(FP4X4),
                lhsT_scale=scales,
                rhs=picked_words[o][:].bitcast(FP8X4),
                rhs_scale=picked_scales[o][:],
                start=opens,
                stop=not opens,
            )

        def leave_psum(t):
            nc.scalar.activation(dec[:, t, :], banks[t, W2][:], ACT.Sigmoid)
            if t == FIRST:
                nc.vector.tensor_scalar(y[t][:], banks[t, W1][:], unit_abs[:, t : t + 1], None, ALU.mult)
            else:
                nc.scalar.activation(y[t][:], banks[t, W1][:], ACT.Copy, scale=unit_abs[:, t : t + 1])

        first_tile = slice(FIRST, FIRST + 1)
        both_weights = slice(0, 2 * PASSES)
        pick_scales()
        pick_words(0)
        deal(slice(0, PASSES), first_tile)
        product_pass(FIRST, W2, 0, True)
        pick_words(1)
        deal(slice(PASSES, 2 * PASSES), first_tile)
        product_pass(FIRST, W1, 0, True)
        for w in (W2, W1):
            product_pass(FIRST, w, 1, False)
        deal(both_weights, slice(2, 3))
        deal(both_weights, slice(0, 2))
        leave_psum(FIRST)
        for t in ORDER[1:]:
            for w in (W2, W1):
                product_pass(t, w, 1, True)
                product_pass(t, w, 0, False)
            leave_psum(t)
        deal_w3()

        out_words = keep.tile([P, S], I32, name="out_words", align_bytes=64)
        out_scales = keep.tile([P, S], U8, name="out_scales", align_bytes=64)
        out_rows = out_0.rearrange("(p t) j -> p t j", t=PACK)
        factor = [keep.tile([P, PACK, HALF], F32, name="factor%d" % h) for h in range(2)]
        m2 = [keep.tile([P, PACK, HALF], F32, name="m2_%d" % h) for h in range(2)]
        up2 = [keep.tile([P, PACK, HALF], F32, name="up2_%d" % h) for h in range(2)]
        x12, x13 = {}, {}
        top, hid, results, result_banks, rounded = {}, {}, {}, {}, {}

        def parent_product(t, h):
            picks = entries(lists["p1"], half(h))
            nc.vector.tensor_tensor(m1[t][:, half(h)], y[t][:].indirect(picks), dec[:, t, half(h)], ALU.mult)

        def first_sum(t):
            nc.vector.tensor_tensor(up1[:, t, :], m1[t][:], y[t][:], ALU.add)

        def fetch(out, window, name, cols):
            nc.scalar.activation(out, window.indirect(entries(lists[name], cols)), ACT.Copy)

        def factor_tile0(h):
            picks = entries(lists["p2"], half(h))
            nc.vector.tensor_tensor(factor[h][:, 0, :], up1_whole[:].indirect(picks), dec[:, 0, half(h)], ALU.mult)

        def factor_others(h):
            nc.vector.tensor_tensor(factor[h][:, 1:, :], dec[:, 1:, half(h)], ap[h][:, 1:, :], ALU.mult)

        def m2_tile0(h):
            picks = entries(lists["p1"], half(h))
            nc.vector.tensor_tensor(m2[h][:, 0, :], dec_whole[:].indirect(picks), factor[h][:, 0, :], ALU.mult)

        def m2_others(h):
            nc.vector.tensor_tensor(m2[h][:, 1:, :], x12[h][:, 1:, :], factor[h][:, 1:, :], ALU.mult)

        def second_sum(h):
            nc.vector.tensor_tensor(up2[h][:], m2[h][:], up1[:, :, half(h)], ALU.add)

        def in_half(c):
            h = PIECES[c].start // HALF
            return h, slice(PIECES[c].start - h * HALF, PIECES[c].stop - h * HALF)

        def width(c):
            return PIECES[c].stop - PIECES[c].start

        def compare(c):
            h, cols = in_half(c)
            top[c] = keep.tile([P, width(c) * PACK], BF16, name="top%d" % c)
            nc.vector.tensor_tensor(
                side_by_side(top[c][:]), in_runs(up2[h][:, :, cols]), in_runs(x13[h][:, :, cols]), ALU.max
            )

        def apply_sign(c):
            hid[c] = keep.tile([P, width(c) * PACK], BF16, name="hid%d" % c, align_bytes=64)
            nc.vector.tensor_tensor(
                hid[c][:].rearrange("p (j t) -> p j t", t=PACK),
                top[c][:].rearrange("p (j t) -> p j t", t=PACK),
                unit_sign[:].unsqueeze(1).to_broadcast([P, width(c), PACK]),
                ALU.mult,
            )

        def last_product(c, tiles_a_bank):
            hid_words = keep.tile([P, width(c)], U32, name="hid_words%d" % c, align_bytes=64)
            hid_scales = keep.tile([P, width(c)], U8, name="hid_scales%d" % c, align_bytes=64)
            nc.vector.quantize_mx(out=hid_words[:].bitcast(FP8X4), scales=hid_scales[:], in_=hid[c][:])
            results[c] = keep.tile([P, PACK, width(c)], F32, name="result%d" % c)
            result_banks[c] = []
            for t0 in range(0, PACK, tiles_a_bank):
                bank = psum.tile([P, tiles_a_bank, width(c)], F32, name="bank")
                for t in range(t0, t0 + tiles_a_bank):
                    nc.tensor.matmul_mx(
                        out=bank[:, t - t0, :],
                        lhsT=w3_dealt_words[:, t, :].bitcast(FP4X4),
                        lhsT_scale=w3_dealt_scales[:, t, :],
                        rhs=hid_words[:].bitcast(FP8X4),
                        rhs_scale=hid_scales[:],
                        start=True,
                        stop=True,
                    )
                result_banks[c].append((results[c][:, t0 : t0 + tiles_a_bank, :], bank))

        def store_result(c):
            for n, (rows, bank) in enumerate(result_banks[c]):
                if c == len(PIECES) - 1 and n == 1:
                    nc.vector.tensor_copy(rows, bank[:])
                else:
                    nc.scalar.activation(rows, bank[:], ACT.Copy)
            nc.sync.dma_start(out=out_rows[:, :, PIECES[c]], in_=results[c][:])

        def round_result(c):
            rounded[c] = keep.tile([P, width(c) * PACK], BF16, name="rounded%d" % c, align_bytes=64)
            nc.vector.tensor_copy(out=side_by_side(rounded[c][:]), in_=in_runs(results[c][:]))

        def hand_on(c):
            cols = PIECES[c]
            nc.vector.quantize_mx(out=out_words[:, cols].bitcast(FP8X4), scales=out_scales[:, cols], in_=rounded[c][:])
            nc.sync.dma_start(
                out=out_1[0].rearrange("p c r -> p (c r)").bitcast(I32)[:, cols], in_=out_words[:, cols]
            )

        for n, t in enumerate(ORDER):
            if t != LAST:
                fetch(ap[0][:, t, :], dec[:, t, :], "p1", half(0))
            parent_product(t, 0)
            if n > 0:
                first_sum(ORDER[n - 1])
            parent_product(t, 1)
        factor_others(0)
        first_sum(LAST)

        x12[0] = keep.tile([P, PACK, HALF], F32, name="x12_0", tag="picked0", align_bytes=64)
        x13[0] = keep.tile([P, PACK, HALF], F32, name="x13_0", tag="picked1", align_bytes=64)
        for t in ORDER[:-1]:
            fetch(x12[0][:, t, :], up1[:, t, :], "p2", half(0))
        for t in ORDER:
            fetch(x13[0][:, t, :], up1[:, t, :], "p3", half(0))
        x12[1] = keep.tile([P, PACK, HALF], F32, name="x12_1", tag="y%d" % LAST)
        ap_and_x13 = keep.tile([P, 2, PACK, HALF], F32, name="ap1_x13_1", tag="m1_%d" % LAST)
        ap[1], x13[1] = ap_and_x13[:, 0], ap_and_x13[:, 1]
        for t in ORDER[:-1]:
            fetch(ap[1][:, t, :], dec[:, t, :], "p1", half(1))
        for t in ORDER[:-1]:
            fetch(x12[1][:, t, :], up1[:, t, :], "p2", half(1))
        for c in (1, 2):
            for t in ORDER:
                fetch(x13[1][:, t, in_half(c)[1]], up1[:, t, :], "p3", PIECES[c])

        factor_tile0(0)
        m2_others(0)
        m2_tile0(0)
        factor_tile0(1)
        second_sum(0)
        m2_tile0(1)
        compare(0)
        factor_others(1)
        apply_sign(0)
        m2_others(1)
        last_product(0, 2)
        store_result(0)
        second_sum(1)
        for step in (compare, apply_sign):
            step(1)
            step(2)
        last_product(1, PACK)
        last_product(2, 2)
        store_result(1)
        round_result(0)
        hand_on(0)
        store_result(2)
        for step in (round_result, hand_on):
            step(1)
            step(2)
        for q in range(QUADRANTS):
            queue = nc.sync if q % 2 == 0 else nc.scalar
            queue.dma_start(
                out=out_2[0, 4 * q : 4 * q + 4, :].bitcast(I32),
                in_=out_scales[32 * q : 32 * q + 4, :].bitcast(I32),
            )
